import numpy as np, ml_dtypes
CORES = [113,118,241,246]
N = 4
BF = ml_dtypes.bfloat16
V, H, LB, K, T, TH = 2048, 1024, 11, 256, 4, 6
ODD = (np.arange(16) & 1)[:, None]
def before(w):
    return np.concatenate([np.zeros_like(w[..., :1, :]), w[..., :-1, :]], axis=-2) * ODD
def follow(rng, cyc):
    F = rng.integers(0, V, (8, 16, V))
    for g in range(8):
        for k in range(16):
            e = np.roll(cyc[g], -(k + 1))
            F[g, k, cyc[g]] = (e + np.roll(cyc[g], -1)) & (V - 1) if k & 1 else e
    return F
def chain(cyc, b):
    return np.take_along_axis(cyc[:, None, :], (b[:, None, :] - np.arange(16)[None, :, None]) % cyc.shape[1], 2)
def spoil(rng, F, share):
    return np.where(rng.random(F.shape) < share, rng.integers(0, V, F.shape), F)
def pack(F, x, w):
    return {"fld": (F[..., :H] + V * F[..., H:]).reshape(N, 128, H).astype(np.int32), "rec": np.ascontiguousarray(x).reshape(N, 128, V).astype(np.float32).astype(BF),
            "wnd": np.ascontiguousarray(w).reshape(N, 128, K).astype(np.int32)}
def setup_inputs(rng):
    cyc = np.argsort(rng.random((8, V)), axis=-1); F = np.stack([follow(rng, cyc)] * N)
    F = spoil(rng, F, rng.choice(np.array([0.12, 0.35, 0.55, 0.68]), (N, 8, 1, 1)))
    w = np.stack([chain(cyc, rng.integers(0, V, (8, K))) for r in range(N)])
    w = spoil(rng, w, rng.choice(np.array([0.0, 0.0, 0.06, 0.06, 0.06, 0.2, 0.2, 1.0]), (N, 8, 1, K)))
    return pack(F, rng.integers(0, 16, (N, 8, 16, V)), w)
def setup_inputs_spread(rng):
    cyc = np.argsort(rng.random((8, V)), axis=-1); F = np.stack([follow(rng, cyc)] * N)
    low = np.minimum((V * rng.random(F.shape) ** 4).astype(np.int64), V - 1)
    F = np.where(rng.random(F.shape) < 0.85 * rng.random((N, 8, 1, 1)) ** 1.5, low, F)
    w = np.stack([chain(cyc, np.minimum((V * rng.random((8, K)) ** 3).astype(np.int64), V - 1)) for r in range(N)])
    w = spoil(rng, w, 0.5 * rng.random((N, 8, 1, K)) ** 3)
    x = np.minimum((16 * rng.random(F.shape) ** np.exp2(rng.integers(-2, 4, (N, 8, 1, V)))).astype(np.int64), 15)
    return pack(F, x, w)
def setup_inputs_ends(rng):
    e = V - 1
    F = e * np.tile(rng.integers(0, 2, (N, 8, 16, H)), (1, 1, 1, 2))
    x = 15 * np.where(rng.random((N, 8, 1, V)) < 0.5, rng.integers(0, 2, (N, 8, 1, V)), rng.integers(0, 2, (N, 8, 16, V)))
    w = e * (rng.random((N, 8, 16, K)) < rng.choice(np.array([0.1, 0.5, 0.9]), (N, 8, 1, K))).astype(np.int64)
    F[:, 4:, :, 0] = 0; F[:, 4:, :, H] = 0; F[:, 4:, :, H - 1] = e; F[:, 4:, :, e] = e
    for c in (0, 1, e):
        x[:, 4, :, c] = 0; x[:, 5, :, c] = 15
    for g in (6, 7):
        x[:, g, :, 0] = 0; x[:, g, :, 1] = 0; x[:, g, :, e] = 15
    x[:, 6, 8:, 1] = 15
    pat = np.zeros((7, 16), np.int64)
    pat[0, 15] = 1; pat[1, 14] = 1; pat[2, 2] = 1; pat[2, 15] = 1; pat[3] = np.array([0, 1] * 7 + [1, 0]); pat[4] = np.array([0, 1] + [1, 0] * 7); pat[5] = 1
    pt = rng.integers(0, 7, (N, 4, K))
    pt[:, 0:2, K - 1] = 4; pt[:, 0:2, 0] = 4; pt[:, 2, K - 1] = 3; pt[:, 2, 1] = 3; pt[:, 3, K - 1] = 0; pt[:, 3, 0] = 2; pt[:, 3, 1] = 6
    pt[N - 1, 3] = 6; pt[N - 1, 3, K - 1] = 0
    w[:, 4:] = e * np.moveaxis(pat[pt], 3, 2)
    return pack(F, x, w)
def setup_inputs_corners(rng):
    R = V // 8; inner = 1 + np.argsort(rng.random((8, V - 2)), axis=-1)
    out = np.concatenate([np.tile(np.array([0, V - 1]), (8, 1)), inner[:, :R - 2]], axis=1); cyc = np.ascontiguousarray(inner[:, R - 2:])
    F = np.stack([follow(rng, cyc)] * N); x = rng.integers(0, 16, (N, 8, 16, V)); s0 = int(rng.integers(0, N)); q = [(s0 + i) % N for i in range(N)]
    b = np.argsort(rng.random((N, 8, V - R)), axis=-1)[..., :K]
    w = np.stack([chain(cyc, b[r]) for r in range(N)])
    for r in (q[1], q[3]):
        F[r] = spoil(rng, F[r], 0.58)
        F[r, :, :, ::16] = 16 * rng.integers(0, V // 16, (8, 16, V // 16)) + np.arange(16)[None, :, None]
        w[r] = 16 * rng.integers(0, V // 16 - 1, (8, 16, K))
    g = int(rng.integers(0, 8)); m = int(rng.integers(0, V))
    w[q[1], g, :, int(rng.integers(0, K))] = V - 16; F[q[1], g, 0::2, V - 16] = m; F[q[1], g, 1::2, V - 16] = (m + V - 16) & (V - 1)
    for r in [q[2]] + q[4:]:
        x[r] = 7 + rng.integers(0, 2, (8, 16, V))
        for h in range(8):
            x[r, h][:, out[h, ::2]] = 0; x[r, h][:, out[h, 1::2]] = 15
        w[r, 3] = cyc[3, b[r, 3]][None, :]; F[r, 3, 0::2] = np.arange(V); F[r, 3, 1::2] = (2 * np.arange(V)) & (V - 1)
        v = rng.choice(np.array([1, TH - 1, TH, TH + 1, 15, 16]), (8, 1, K)); o = np.argsort(rng.random((8, 16, K)), axis=1)
        y = np.take_along_axis(out[:, None, :], (rng.integers(0, R, (8, 1, K)) + o) % R, 2)
        new = (y + before(w[r])) & (V - 1); old = np.take_along_axis(F[r], w[r], 2)
        np.put_along_axis(F[r], w[r], np.where(o >= v, new, old), 2)
    return pack(F, x, w)
def setup_inputs_crowd(rng):
    cyc = np.argsort(rng.random((8, V)), axis=-1); F = np.stack([follow(rng, cyc)] * N)
    a = int(rng.integers(0, N)); e = (a - 1) % N; p = (a + 1) % N; q = (a + 2) % N
    share = np.tile(np.array([0.0, 0.0, 0.1, 0.0, 0.0, 0.1, 0.1, 0.3]).reshape(1, 8, 1, 1), (N, 1, 1, 1))
    for r in (e, a, p, q): share[r, 7] = 0.0
    share[p] = 0.0; share[q] = 0.0
    F = spoil(rng, F, share)
    x = rng.integers(0, 8, (N, 8, 16, V)); x[:, 7] = rng.integers(0, 16, (N, 16, V))
    b = rng.integers(64, V - 64, (N, 8, K))
    b[:, 3] = 64 + np.argsort(rng.random((N, V - 128)), axis=-1)[:, :K]
    b[:, 7] = H + 64 + np.argsort(rng.random((N, H - 128)), axis=-1)[:, :K]; b[a, 7] = b[a, 7] - H
    w = np.stack([chain(cyc, b[r]) for r in range(N)])
    for g in (0, 1, 2, 4, 5, 6):
        bad = cyc[g, :3]; o = int(cyc[g, 4]); x[:, g, :, o] = 15
        for c in bad: F[:, g, 0::2, c] = o
        for r in range(N):
            if r == p: continue
            k = 2 * rng.integers(0, 8, K); c = bad[rng.integers(0, 3, K)] if g == 6 else np.full(K, bad[0]); j = np.arange(K)
            if g in (4, 5): j = np.delete(j, int(rng.integers(0, K)))
            w[r, g, k[j], j] = c[j]
    o = int(cyc[3, 4]); x[:, 3, :, o] = 15; k0 = int(rng.integers(0, 16))
    for r in range(N):
        k = (k0 + 5 * r) % 16
        F[r, 3, k, w[r, 3, k]] = (o + before(w[r, 3])[k]) & (V - 1)
    out = cyc[7, 8:40]
    for r, whose, t in ((a, e, 1), (q, a, 2)):
        x[r, 7] = 7 + rng.integers(0, 2, (16, V)); x[r, 7][:, out[::2]] = 0; x[r, 7][:, out[1::2]] = 15
        then = chain(cyc[7:], b[whose, 7][None, :] + t)[0]
        v = rng.choice(np.array([TH - 1, TH, TH, TH + 1]), (1, K)); turn = np.argsort(rng.random((16, K)), axis=0)
        y = out[(rng.integers(0, 32, (1, K)) + turn) % 32]
        new = (y + before(then)) & (V - 1); old = np.take_along_axis(F[r, 7], then, 1)
        np.put_along_axis(F[r, 7], then, np.where(turn >= v, new, old), 1)
    for g in (2, 5): w[a, g] = rng.integers(0, V, (16, K))
    w[q, 7, :, int(rng.integers(0, K))] = rng.integers(0, V, 16)
    return pack(F, x, w)
def setup_inputs_ties(rng):
    cyc = np.argsort(rng.random((8, V)), axis=-1); F = np.stack([follow(rng, cyc)] * N)
    r0 = int(rng.integers(0, N)); r1 = (r0 + 1) % N; r2 = (r0 + 2) % N
    sf = rng.choice(np.array([0.05, 0.2, 0.45]), (N, 8, 1, 1)); sw = rng.choice(np.array([0.0, 0.05, 0.2]), (N, 8, 1, K))
    for s in (sf, sw):
        s[r1] = 0.0; s[r2] = 0.0; s[r0, 6:] = 0.0
    F = spoil(rng, F, sf)
    b = rng.integers(0, V, (N, 8, K))
    b[:, 6:] = H + 64 + np.argsort(rng.random((N, 2, H - 128)), axis=-1)[..., :K]; b[r0, 6:] = b[r0, 6:] - H
    w = np.stack([chain(cyc, b[r]) for r in range(N)]); w = spoil(rng, w, sw)
    kind = rng.integers(0, 4, (N, 8, 1, V)); kind[:, 0] = 0
    x = np.take_along_axis(rng.integers(0, 16, (N, 8, 16, 4)), kind, 3)
    w[r1, int(rng.integers(0, 6)), :, int(rng.integers(0, K))] = rng.integers(0, V, 16)
    two = chain(cyc[7:], b[r1, 7, rng.permutation(K)[:2]][None, :] + 1)[0]
    np.put_along_axis(F[r2, 7], two, rng.integers(0, V, (16, 2)), 1)
    for r, g, t in ((r1, 7, 1), (r2, 6, 2)):
        out = cyc[g, 8:40]
        x[r, g] = (7 + rng.integers(0, 2, (16, 4)))[:, kind[r, g, 0]]; x[r, g][:, out[::2]] = 0; x[r, g][:, out[1::2]] = 15
        then = chain(cyc[g:g + 1], b[r0, g][None, :] + t)[0]
        v = rng.choice(np.array([TH - 1, TH, TH, TH + 1]), (1, K)); turn = np.argsort(rng.random((16, K)), axis=0)
        y = out[(rng.integers(0, 32, (1, K)) + turn) % 32]
        new = (y + before(then)) & (V - 1); old = np.take_along_axis(F[r, g], then, 1)
        np.put_along_axis(F[r, g], then, np.where(turn >= v, new, old), 1)
    return pack(F, x, w)
def check_inputs(d):
    bad = []
    for k, hi in (("fld", V * V - 1), ("rec", 15), ("wnd", V - 1)):
        v = np.asarray(d[k]).astype(np.float64)
        if not (np.all(v >= 0) and np.all(v <= hi)): bad.append("range of " + k)
    v = np.asarray(d["rec"]).astype(np.float64)
    if not np.all(v == np.floor(v)): bad.append("whole numbers in rec")
    return bad
def reference(fld, rec, wnd):
    pk = fld.astype(np.int64).reshape(N, 8, 16, H); F = np.concatenate([pk & (V - 1), pk >> LB], axis=3)
    X = rec.astype(np.float32).astype(np.int64).reshape(N, 8, 16, V)
    here = [a for a in wnd.astype(np.int64).reshape(N, 8, 16, K)]
    A = np.zeros(N, np.int64); wt = (2 * np.arange(16) + 1)[None, :, None]
    for t in range(T):
        left = []
        for q in range(N):
            w = here[q]; pv = before(w)
            e = (np.take_along_axis(F[q], w, 2) - pv) & (V - 1)
            x = np.take_along_axis(X[q], e.reshape(8, 1, 16 * K), 2).reshape(8, 16, 16, K)
            M = np.add.reduce(x, axis=2) >> 4
            d = np.add.reduce(np.abs(x - M[:, :, None, :]), axis=1)
            lo = np.argmin(d, axis=1)[:, None, :]; hi = np.argmax(d, axis=1)[:, None, :]
            n = np.take_along_axis(e, lo, 1)
            s = np.add.reduce((e == n).astype(np.int64), axis=1)
            go = s >= TH + (A[q] & 1)
            want = go & (np.take_along_axis(e, hi, 1) != n)[:, 0]
            col = np.take_along_axis(w, hi, 1)[:, 0]; val = ((n + np.take_along_axis(pv, hi, 1)) & (V - 1))[:, 0]
            for g in range(8):
                i = np.flatnonzero(want[g]); c, first = np.unique(col[g, i], return_index=True); i = i[first]
                F[q, g, hi[g, 0, i], c] = val[g, i]
            u = np.add.reduce(M * wt, axis=1); z = ((u * u >> 5) + 37 * u) & (V - 1)
            A[q] = np.count_nonzero(~go)
            left.append(np.where(go[:, None, :], np.concatenate([n, w[:, :15]], axis=1), np.concatenate([z[:, None, :], w[:, 14::-1]], axis=1)))
        here = left if t == T - 1 else [left[(q - 1) % N] for q in range(N)]
    return {"yf": (F[..., :H] + V * F[..., H:]).reshape(N, 128, H).astype(np.float32), "yw": np.stack(here).reshape(N, 128, K).astype(np.float32)}

@@ -1,0 +1,575 @@
+from concourse.mybir import AluOpType as A, ActivationFunctionType as AF
+
+NV = 4
+FO = 32
+MAGIC = 1.5 * 2.0 ** 34
+
+SCRATCH = {
+    "fin": ("sbuf", [128, 1024], "int32"), "wi": ("sbuf", [128, 256], "int32"),
+    "Y": ("sbuf", [128, 1024], "float32"), "F": ("sbuf", [128, FO + 2064], "int32"),
+    "rec2": ("sbuf", [128, 4096], "bfloat16"),
+    "G": ("sbuf", [128, 4096], "float16"), "X": ("sbuf", [128, 4096], "bfloat16"), "MX": ("sbuf", [128, 4096], "bfloat16"),
+    "WO": ("sbuf", [128, 256 * NV], "uint16"), "WF": ("sbuf", [128, 256 * NV], "float16"),
+    "SO": ("sbuf", [128, 256 * NV], "uint16"), "SF": ("sbuf", [128, 256 * NV], "float16"),
+    "YW": ("sbuf", [128, 256], "float32"),
+    "EO": ("sbuf", [128, 256], "uint16"), "VT": ("sbuf", [128, 256], "float16"), "NG": ("sbuf", [128, 256], "bfloat16"),
+    "TT": ("sbuf", [128, 1536], "float16"), "MO": ("sbuf", [128, 768], "float16"),
+    "MB": ("sbuf", [128, 256], "bfloat16"), "KS": ("sbuf", [128, 1024], "int32"), "SS": ("sbuf", [128, 256], "float32"),
+    "PL": ("sbuf", [128, 80], "int32"), "SM": ("sbuf", [128, 64], "float32"),
+    "T1": ("sbuf", [128, 16], "int32"), "T2": ("sbuf", [128, 16], "int32"), "T3": ("sbuf", [128, 16], "float32"),
+    "T4": ("sbuf", [128, 16], "float32"),
+    "U2": ("sbuf", [128, 16], "float32"), "Z1": ("sbuf", [128, 16], "int32"), "ZI": ("sbuf", [128, 16], "int32"),
+    "ZT": ("sbuf", [128, 256], "float16"), "BM": ("sbuf", [128, 512], "float32"), "EQ": ("sbuf", [128, 512], "bfloat16"),
+    "LG": ("sbuf", [128, 16], "uint16"),
+    "OLD": ("sbuf", [128, 256], "float16"), "DL": ("sbuf", [128, 256], "int32"),
+    "AJ": ("sbuf", [128, 16], "float32"), "AS": ("sbuf", [128, 1], "float32"), "AI": ("sbuf", [128, 1], "int32"),
+    "AP1": ("sbuf", [128, 1], "int32"), "PAR": ("sbuf", [128, 1], "float32"),
+    "ONE": ("sbuf", [128, 128], "bfloat16"), "NONE": ("sbuf", [128, 128], "bfloat16"), "ONEF": ("sbuf", [128, 128], "float32"),
+    "ID": ("sbuf", [128, 128], "bfloat16"), "NID": ("sbuf", [128, 128], "bfloat16"),
+    "ODD": ("sbuf", [128, 128], "bfloat16"), "NODD": ("sbuf", [128, 128], "bfloat16"),
+    "SH": ("sbuf", [128, 128], "bfloat16"), "NSH": ("sbuf", [128, 128], "bfloat16"),
+    "KEEP": ("sbuf", [128, 128], "bfloat16"), "SHF": ("sbuf", [128, 128], "bfloat16"), "REV": ("sbuf", [128, 128], "bfloat16"),
+    "DR": ("sbuf", [128, 128], "bfloat16"), "BL0": ("sbuf", [128, 256], "bfloat16"), "BLK": ("sbuf", [128, 256], "bfloat16"),
+    "PS0": ("sbuf", [128, 144], "bfloat16"), "PS1": ("sbuf", [128, 144], "bfloat16"), "PS": ("sbuf", [128, 144], "bfloat16"),
+    "IK": ("sbuf", [128, 128], "bfloat16"), "KC": ("sbuf", [128, 512], "bfloat16"), "N192": ("sbuf", [128, 512], "bfloat16"),
+    "RST": ("sbuf", [128, 512], "bfloat16"), "TRI": ("sbuf", [128, 256], "bfloat16"), "WT": ("sbuf", [128, 8], "bfloat16"),
+    "PI": ("sbuf", [128, 1], "int32"), "PI2": ("sbuf", [128, 2], "int32"), "PLO": ("sbuf", [128, 1], "float32"),
+    "NQ": ("sbuf", [128, 2], "float32"), "W2": ("sbuf", [128, 1], "float32"), "PQ": ("sbuf", [128, 2], "float32"),
+    "BLI": ("sbuf", [128, 40], "int32"), "BL": ("sbuf", [128, 40], "uint16"),
+    "B31": ("sbuf", [128, 8], "bfloat16"), "B32": ("sbuf", [128, 8], "bfloat16"), "F0": ("sbuf", [128, FO + 2064], "int32"),
+    "B30": ("sbuf", [128, 8], "bfloat16"), "C31": ("sbuf", [128, 8], "bfloat16"), "LO": ("sbuf", [128, 16], "uint16"),
+    "bK0": ("psum", [128, 512], "float32"), "bK1": ("psum", [128, 512], "float32"), "bM": ("psum", [128, 512], "float32"),
+    "bR0": ("psum", [128, 512], "float32"), "bR1": ("psum", [128, 512], "float32"), "bV": ("psum", [128, 512], "float32"),
+    "bS": ("psum", [128, 512], "float32"), "bT": ("psum", [128, 512], "float32"),
+}
+SEMAPHORES = (["cV", "cA", "cP", "cG", "sent"] + ["arr%s%d%d" % (k, t, c) for k in "OF" for t in range(1, NV) for c in range(2)]
+              + ["dma%d" % i for i in range(15)])
+
+CFG = {
+    "pos": {}, "FG": {1: "AAAAVVVV", 0: "AA AA VV VV"}, "XG": {1: "AA AA VV VV", 0: "AA AA AA AA"}, "MN": {1: "VVVV", 0: "VAVA"},
+    "MO": {1: "VVV", 0: "VVV"}, "EQ": {1: "V", 0: "V"},
+    "Z1": {1: "A", 0: "A"}, "ZT": {1: "A", 0: "A"}, "LO": {1: "A", 0: "A"}, "SO": {1: "A", 0: "A"}, "EO": {1: "V", 0: "V"},
+    "TO": {1: 0, 0: 1}, "VS": {1: 4, 0: 1}, "VE": {1: "V", 0: "A"},
+    "gam": 1.56, "sig": 3.5, "pe": 0.45, "wake": 70.0, "same": True, "look": 0.02, "seed": 0, "noise": 0.0,
+}
+CFG.update({'FG': {1: 'AA AA VVVV', 0: 'AA AAAVVV'}, 'XG': {1: 'A V AA VAVV', 0: 'VA AV AAA V'}, 'MN': {1: 'VVVV', 0: 'AAAA'}, 'MO': {1: 'VVA', 0: 'VVA'}, 'EQ': {1: 'A', 0: 'V'}, 'TO': {1: 0, 0: 0}, 'VS': {1: 4, 0: 1}, 'VE': {1: 'V', 0: 'A'}})
+PLACES = """1235 1444 1219 28 5 344 126 787 246 317 299 367 333 388 998 913 106 1095 999 352 497 425 1065 985 239 50 996 1092 1254 1057 1038 1048 1093 1062 -54 158 177 220 230 414 394 390 178 338 353 33 136 54 52 871 758 1116 1020 944 908 697 566 1032 967 881 886 884 883 860 728 769 853 657 727 597 596 -31 502 422 321 -3 12 733 813 -42 68 1044 957 -17 1002 29 1625 268 474 441 929 807 917 766 500 750 589 312 49 103 138 -122 70 -138 16 -139 215 17 308 113 292 1236 909 30 96 1091 956 988 866 952 803 968 822 989 863 1031 885 879 732 1006 823 618 530 421 738 763 848 955 859 876 751 442 345 588 1076 912 112 1124 1001 120 656 513 565 585 590 610 514 436 473 521 456 439 451 260 145 90 141 1201 962 889 705 931 689 8 963 717 1105 954 1015 970 200 887 888 851 882 875 393 1021 283 902 838 904 247 579 672 663 592 595 302 531 529 594 593 135 768 581 27 796 170 325 839 396 806 318 391 245 212 281 707 256 789 587 501 643 518 1139 1148 868 601 910 924 1047 987 759 458 364 673 586 447 1045 890 981 858 -9 -62 1007 880 53 51 -41 250 243 275 242 1159 965"""
+
+
+def parts(text):
+    out, at = [], 0
+    for word in text.split():
+        for i, ch in enumerate(word):
+            if i and ch == word[i - 1]:
+                out[-1][2] += 1
+            else:
+                out.append([ch, at, at + 1])
+            at += 1
+    return out
+
+
+def build(g, T, topo, core, cfg):
+    ops = []
+    V, S, PE = g.vector, g.scalar, g.tensor
+    gam, sig, pe = cfg["gam"], cfg["sig"], cfg["pe"]
+    ndma, now = [0], [-1]
+
+    def op(q, fn, rd, wr, cost, banks=(), lat=0.0, sem=None, cnt=0):
+        ops.append({"q": q, "fn": fn, "rd": list(rd), "wr": list(wr), "cost": cost, "banks": list(banks), "lat": lat,
+                    "sem": sem, "cnt": cnt, "t": now[0]})
+
+    def v(fn, rd, wr, n, banks=()):
+        op("V", fn, rd, wr, 50 + 0.83 * n, banks)
+
+    def a(fn, rd, wr, n, banks=()):
+        op("A", fn, rd, wr, 65 + 0.83 * n, banks)
+
+    def gp(fn, rd, wr, n):
+        op("G", fn, rd, wr, 170 + 1.66 * n)
+
+    def mm(lst, rd, wr, bank, least=64, group=None):
+        close = [False]
+
+        def fn():
+            r = None
+            for i, (o, l, rh, st, sp, n) in enumerate(lst):
+                r = PE.matmul(o, l, rh, st, sp or (close[0] and i == len(lst) - 1))
+            return r
+        op("P", fn, rd, wr, sum(max(least, m[5]) * pe + 5 for m in lst), [bank])
+        ops[-1]["group"], ops[-1]["close"] = group, close
+
+    def dma(q, out, in_, rd, wr, lat):
+        e = {"S": g.sync, "A": g.scalar}[q]
+        op(q, lambda: e.dma_start(out, in_), rd, wr, 60, (), lat, "dma%d" % ndma[0], 16)
+        ndma[0] += 1
+
+    def ts(o, i, s1, s2, o0, o1=None):
+        if o1 is None:
+            return lambda: V.tensor_scalar(o, i, s1, None, o0)
+        return lambda: V.tensor_scalar(o, i, s1, s2, o0, o1)
+
+    def tt(o, i0, i1, o0):
+        return lambda: V.tensor_tensor(o, i0, i1, o0)
+
+    def cp(o, i):
+        return lambda: V.tensor_copy(o, i)
+
+    def ms(o, c):
+        return lambda: V.memset(o, c)
+
+    def act(o, i, f, **kw):
+        return lambda: S.activation(o, i, f, **kw)
+
+    def sel(o, i, pat, cmp, base, cm):
+        return lambda: g.affine_select(o, i, pat, cmp, 0.0, base, cm)
+
+    def iota(o, pat, base, cm, flag=True):
+        if flag:
+            return lambda: g.iota(o, pat, base, cm, allow_small_or_imprecise_dtypes=True)
+        return lambda: g.iota(o, pat, base, cm)
+
+    dma("S", T.wi[:], T.wnd[:], [], ["wi", "q0"], 2000)
+    dma("A", T.fin[:, 0:512], T.fld[:, 0:512], [], ["fin0"], 2500)
+    dma("S", T.fin[:, 512:1024], T.fld[:, 512:1024], [], ["fin1"], 3000)
+    dma("S", T.rec2[:, 0:2048], T.rec[:], [], ["rec0"], 4200)
+    dma("S", T.rec2[:, 2048:4096], T.rec[:], [], ["rec1"], 5400)
+    v(ms(T.ONE[:], 1.0), [], ["ONE"], 64)
+    v(ms(T.NONE[:], -1.0), [], ["NONE"], 64)
+    v(ms(T.ONEF[:], 1.0), [], ["ONEF"], 128)
+    v(ms(T.F[:, 0:FO], 0), [], ["Fd"], 32)
+    v(ms(T.PAR[:], 0.0), [], ["PAR"], 8)
+    v(ms(T.N192[:], -192.0), [], ["N192"], 256)
+    v(ms(T.ZT[:], 0.0), [], ["ZT0", "ZT1"], 128)
+    for i, (lo, hi, val) in enumerate([(0, 8, 1.0), (8, 32, -1.0), (32, 40, -2.0), (40, 64, 2.0), (64, 72, -1.0), (72, 96, 1.0),
+                                       (96, 104, 2.0), (104, 128, -2.0), (128, 136, -1.0 / 16), (136, 144, 2.0 ** -16)]):
+        v(ms(T.PS0[:, lo:hi], val * 65536.0), [], ["PS0.%d" % i], 8)
+    gp(sel(T.ID[:], T.ONE[:], [[-1, 128]], A.is_equal, 0, 1), ["ONE"], ["ID"], 128)
+    gp(iota(T.NODD[:], [[0, 64], [-1, 2]], 0, 0), [], ["NODD"], 128)
+    gp(sel(T.NSH[:], T.NODD[:], [[-1, 128]], A.is_equal, 1, 1), ["NODD"], ["NSH"], 128)
+    gp(iota(T.IK[:], [[0, 8], [1, 16]], 0, 0), [], ["IK"], 128)
+    gp(iota(T.PI[:], [[0, 1]], 0, 1, False), [], ["PI"], 1)
+    gp(iota(T.BLI[:, 0:24], [[1, 24]], 0, 0, False), [], ["BLI"], 24)
+    gp(iota(T.KC[:], [[0, 32], [4096, 16]], 0, 0), [], ["KC"], 512)
+    gp(sel(T.NID[:], T.NONE[:], [[-1, 128]], A.is_equal, 0, 1), ["NONE"], ["NID"], 128)
+    gp(sel(T.KEEP[:], T.ONE[:], [[0, 8], [1, 16]], A.is_gt, 0, 0), ["ONE"], ["KEEP"], 128)
+    gp(sel(T.SHF[:], T.KEEP[:], [[-1, 128]], A.is_equal, 1, 1), ["KEEP"], ["SHF"], 128)
+    gp(sel(T.REV[:], T.KEEP[:], [[-16, 8], [1, 16]], A.is_equal, -15, 1), ["KEEP"], ["REV"], 128)
+    gp(sel(T.PS1[:], T.PS0[:], [[0, 18], [-16, 8]], A.is_ge, 0, 1), ["PS0.%d" % i for i in range(10)], ["PS1"], 144)
+    gp(sel(T.PS[:], T.PS1[:], [[0, 18], [16, 8]], A.is_ge, 15, -1), ["PS1"], ["PS"], 144)
+    v(ts(T.ODD[:], T.ID[:], -1.0, 1.0, A.mult, A.add), ["ID"], ["ODD"], 64)
+    v(ms(T.C31[:], FO - 1.0), [], ["C31"], 8)
+    v(ms(T.B30[:, 0:4], -4096.0), [], ["B30a"], 8)
+    v(ms(T.B30[:, 4:8], 4096.0), [], ["B30b"], 8)
+    v(ms(T.F[:, FO + 2048:FO + 2064], 0), [], ["Fe"], 8)
+    for h in range(2):
+        s = slice(128 * h, 128 * h + 128)
+        gp(sel(T.BL0[:, s], T.ODD[:], [[-32, 4], [0, 32]], A.is_ge, -16 * h, 1), ["ODD"], ["BL0%d" % h], 128)
+        gp(sel(T.BLK[:, s], T.BL0[:, s], [[32, 4], [0, 32]], A.is_ge, 16 * h + 15, -1), ["BL0%d" % h], ["BLK%d" % h], 128)
+    gp(sel(T.B31[:], T.B30[:], [[0, 2], [-32, 4]], A.is_ge, 0, 1), ["B30a", "B30b"], ["B31"], 8)
+    gp(sel(T.B32[:], T.B31[:], [[0, 2], [32, 4]], A.is_ge, 31, -1), ["B31"], ["B32"], 8)
+    v(ts(T.SH[:], T.NSH[:], -1.0, None, A.mult), ["NSH"], ["SH"], 64)
+    v(ts(T.PI2[:, 0:1], T.PI[:], 15, None, A.bitwise_and), ["PI"], ["PI2"], 8)
+    v(ts(T.PI2[:, 1:2], T.PI[:], 31, None, A.bitwise_and), ["PI"], ["PI3"], 8)
+    v(cp(T.PLO[:], T.PI2[:, 0:1]), ["PI2"], ["PLO"], 8)
+    v(ts(T.W2[:], T.PLO[:], 2.0, 1.0, A.mult, A.add), ["PLO"], ["W2"], 8)
+    v(ts(T.WT[:], T.PS[:, 136:144], T.W2[:], None, A.mult), ["PS", "W2"], ["WT"], 8)
+    for h in range(2):
+        v(ts(T.NQ[:, h:h + 1], T.PLO[:], 2.0 * h - 1, FO - 1.0 + 2049 * h, A.mult, A.add), ["PLO"], ["NQ%d" % h], 8)
+        v(ts(T.PQ[:, h:h + 1], T.PI2[:, 1:2], -16.0 * h, None, A.add), ["PI3"], ["PQ%d" % h], 8)
+        v(ts(T.TRI[:, 128 * h:128 * h + 128], T.IK[:], T.PQ[:, h:h + 1], 4096.0, A.is_lt, A.mult), ["IK", "PQ%d" % h], ["TRI%d" % h], 64)
+    gp(iota(T.BLI[:, 24:40], [[0, 2], [1, 8]], 0, 0, False), [], ["BLI2"], 16)
+    v(cp(T.BL[:], T.BLI[:]), ["BLI", "BLI2"], ["BL"], 40)
+    v(tt(T.DR[:], T.SHF[:], T.REV[:], A.subtract), ["SHF", "REV"], ["DR"], 256)
+    v(ts(T.RST[:], T.KC[:], 0.0, 2.0 ** 25, A.is_equal, A.mult), ["KC"], ["RST"], 256)
+    for c in (0, 1):
+        v(cp(T.TT[:, 768 * c:768 * c + 128], T.IK[:]), ["IK"], ["TTk%d" % c], 64)
+        v(ts(T.TT[:, 768 * c + 384:768 * c + 512], T.IK[:], T.PLO[:], None, A.is_equal), ["IK", "PLO"], ["TTm%d" % c], 64)
+    for h in range(2):
+        s = slice(512 * h, 512 * h + 512)
+        a(act(T.F[:, FO + 1024 + 512 * h:FO + 1536 + 512 * h], T.fin[:, s], AF.Identity, bias=-1023.5 / 2048, scale=1.0 / 2048),
+          ["fin%d" % h], ["Fh%d" % h], 512)
+        v(ts(T.F[:, FO + 512 * h:FO + 512 * h + 512], T.fin[:, s], 2047, None, A.bitwise_and), ["fin%d" % h], ["Fl%d" % h], 512)
+    v(cp(T.WO[:, 0:256], T.wi[:]), ["wi"], ["WO01", "WO00"], 256)
+    a(act(T.WF[:, 0:256], T.wi[:], AF.Copy), ["wi"], ["WF01", "WF00"], 256)
+    FK = ["Fd", "Fe", "Fh0", "Fh1", "Fl0", "Fl1"]
+    rank = T.rank_of(core)
+    dst = T.cores[(rank + 1) % len(T.cores)]
+    rid, pid = topo.addr(dst, core)
+    mask = topo.mask(core, dst)
+
+    def plus(kind, c, out, in_, add, rd, wr, n, banks=()):
+        if cfg[kind][c] == "A":
+            a(act(out, in_, AF.Identity, bias=add) if add else act(out, in_, AF.Copy), rd, wr, n, banks)
+        else:
+            v(ts(out, in_, add, None, A.add) if add else cp(out, in_), rd, wr, n, banks)
+
+    def gather(who, out, win, rd, wr, n):
+        if who == "V":
+            v(cp(out, win), rd, wr, gam * n)
+        else:
+            a(act(out, win, AF.Copy), rd, wr, gam * n)
+
+    for t in range(NV):
+        now[0] = t
+        dma("S", T.F0[:], T.F[:], FK + ["rec0", "rec1", "WF%d0" % t], ["F0"], 6000)
+        for c in (1, 0):
+            for who, lo, hi in parts(cfg["FG"][c]):
+                w0 = 256 * t + 128 * c
+                gather(who, T.G[:, 2048 * c + 256 * lo:2048 * c + 256 * hi], T.F[:, FO:FO + 2048].indirect(T.WO[:, w0 + 16 * lo:w0 + 16 * hi]),
+                       FK + ["WO%d%d" % (t, c)], ["G%d.%d" % (c, s) for s in range(lo, hi)], 256 * (hi - lo))
+        for c in (1, 0):
+            C = str(c)
+            w0 = 256 * t + 128 * c
+            x0 = 128 * c
+            WFk, WOk = "WF%d%d" % (t, c), "WO%d%d" % (t, c)
+            Wf = T.WF[:, w0:w0 + 128]
+            bK = T["bK" + C]
+            TT0 = 768 * c
+            g0 = 2048 * c
+            Gk = ["G%d.%d" % (c, s) for s in range(8)]
+            Xk = ["X%d.%d" % (c, s) for s in range(8)]
+            b = "bR" + C
+            mm([(T[b][:, 0:128], Wf, T.NSH[:], True, False, 128)], [WFk, "NSH"], [b], b)
+            vs = cfg["VS"][c]
+            for s in range(vs):
+                m = 128 // vs
+                mm([(T[b][m * s:m * s + m, k:128:16], T.G[:, g0 + 16 * m * s + k:g0 + 16 * m * (s + 1):16], T.ID[:, k:128:16], False,
+                     k == 15, 8) for k in range(16)], Gk[8 // vs * s:8 // vs * (s + 1)] + ["ID"], [b], b, min(m, 64))
+            VT = T.VT[:, x0:x0 + 128]
+            if cfg["VE"][c] == "A":
+                a(act(VT, T[b][:, 0:128], AF.Copy), [b], ["VT" + C], 128, [b])
+            else:
+                v(cp(VT, T[b][:, 0:128]), [b], ["VT" + C], 128, [b])
+            mm([(T.bV[:, 128:256], VT, T.ID[:], True, True, 128)], ["VT" + C, "ID"], ["bVb"], "bV")
+            plus("EO", c, T.EO[:, x0:x0 + 128], T.bV[:, 128:256], 2048.0, ["bVb"], ["EO" + C], 128, ["bV"])
+            for who, lo, hi in parts(cfg["XG"][c]):
+                gather(who, T.X[:, g0 + 256 * lo:g0 + 256 * hi], T.rec2[:, 0:4096].indirect(T.EO[:, x0 + 16 * lo:x0 + 16 * hi]),
+                       ["rec0", "rec1", "EO" + C], Xk[lo:hi], 256 * (hi - lo))
+            v(ts(T.NG[:, x0:x0 + 128], VT, 0.0, 2048.0, A.is_lt, A.mult), ["VT" + C], ["NG" + C], 64)
+            mm([(T.bV[:, 256:384], T.ID[:], VT, True, False, 128), (T.bV[:, 256:384], T.ID[:], T.NG[:, x0:x0 + 128], False, True, 128),
+                (T.bV[:, 384:512], Wf, T.DR[:], True, True, 128)], ["VT" + C, "NG" + C, WFk, "DR", "ID"], ["bVc"], "bV")
+            a(act(T.TT[:, TT0 + 128:TT0 + 384], T.bV[:, 256:512], AF.Copy), ["bVc"], ["TTe" + C, "TTd" + C], 256, ["bV"])
+            BK = "bK" + C
+            mm([(bK[:], T.ONE[0:1, :], T.KC[0:1, :], True, False, 512), (bK[:, 256:384], T.ONE[0:1, :], T.ONE[0:1, :], False, False, 128)],
+               ["ONE", "KC"], [BK], BK)
+            mm([(bK[:, 128:256], Wf, T.SH[:], False, False, 128), (bK[:, 256:384], Wf, T.ID[:], False, False, 128),
+                (bK[:, 384:512], Wf, T.SH[:], False, False, 128)], [WFk, "SH", "ID", BK], [BK + "w"], BK, group=(t, c))
+            mm([(bK[:, 128:256], T.ID[:], VT, False, False, 128), (bK[:, 0:128], T.ID[:], T.TT[:, TT0 + 128:TT0 + 256], False, False, 128)],
+               ["TTe" + C, "VT" + C, "ID", BK], [BK + "e"], BK, group=(t, c))
+        for c in (1, 0):
+            C = str(c)
+            w0 = 256 * t + 128 * c
+            x0 = 128 * c
+            WFk = "WF%d%d" % (t, c)
+            BK = "bK" + C
+            Wf = T.WF[:, w0:w0 + 128]
+            bK = T["bK" + C]
+            TT0 = 768 * c
+            g0 = 2048 * c
+            Xk = ["X%d.%d" % (c, s) for s in range(8)]
+            for h in range(2):
+                mm([(T.bS[:, 64 * h:64 * h + 64], T.ID[:], T.X[:, g0 + 1024 * h + k:g0 + 1024 * h + 1024:16], k == 0, k == 15, 64)
+                    for k in range(16)], Xk[4 * h:4 * h + 4] + ["ID"], ["bS%d" % h], "bS")
+            MB = T.MB[:, x0:x0 + 128]
+            a(act(MB, T.bS[:, 0:128], AF.Identity, bias=192.0 - 15.0 / 32, scale=1.0 / 16), ["bS0", "bS1"], ["MB" + C], 128, ["bS"])
+            mn = cfg["MN"][c]
+            if "V" in mn:
+                mm([(T.bM[:], T.ONE[0:1, :], T.N192[0:1, :], True, False, 512)], ["ONE", "N192"], ["bM"], "bM")
+                mm([(T.bM[:, s:512:4], T.ID[:], MB, False, s == 3, 128) for s in range(4)], ["MB" + C, "ID"], ["bM"], "bM")
+            nr = 0
+            for j in range(4):
+                Xj = T.X[:, g0 + j:g0 + 2048:4]
+                MXj = T.MX[:, g0 + 512 * j:g0 + 512 * j + 512]
+                MXk = "MX%d.%d" % (c, j)
+                if mn[j] == "V":
+                    v(tt(MXj, Xj, T.bM[:], A.min), Xk + ["bM"], [MXk], 512, ["bM"])
+                else:
+                    b = (["bR0", "bR1"] * 2 if c else ["bR0", "bR1", "bV", "bM"])[nr]
+                    bk = ["bVb", "bVc"] if b == "bV" else [b]
+                    nr += 1
+                    mm([(T[b][:], T.ID[:], Xj, True, False, 512)], Xk + ["ID"], bk, b)
+                    mm([(T[b][:, s:512:4], T.NID[:], MB, False, s == 3, 128) for s in range(4)], ["MB" + C, "NID"], bk, b)
+                    a(act(MXj, T[b][:], AF.Relu if "V" in mn else AF.Abs, bias=192.0), bk, [MXk], 512, [b])
+            for j in range(4 if "V" in mn else 0):
+                mm([(bK[:, k:512:16], T.X[:, g0 + k:g0 + 2048:16], T.PS[:, 0:32] if mn[j] == "V" else T.PS[:, 64:96], False, False, 32)
+                    for k in range(j, 16, 4)], Xk + ["PS", BK], [BK + "x%d" % j], BK, group=(t, c))
+            mm([(T.bS[:, 128:136], MB, T.WT[:], True, True, 8)], ["MB" + C, "WT"], ["bSu"], "bS")
+            c8 = slice(8 * c, 8 * c + 8)
+            a(act(T.U2[:, c8], T.bS[:, 128:136], AF.Square, bias=592.0 - 192.0 * 256), ["bSu"], ["U2" + C], 8, ["bS"])
+            plus("Z1", c, T.Z1[:, c8], T.U2[:, c8], 42752.0, ["U2" + C], ["Z1" + C], 8)
+            v(ts(T.ZI[:, c8], T.Z1[:, c8], 5, 2047, A.arith_shift_right, A.bitwise_and), ["Z1" + C], ["ZI" + C], 8)
+            plus("ZT", c, T.ZT[:, x0:x0 + 128:16], T.ZI[:, c8], 0.0, ["ZI" + C], ["ZT" + C], 8)
+            for j in range(4):
+                mm([(bK[:, j + 4 * kk:512:16], T.MX[:, g0 + 512 * j + kk:g0 + 512 * j + 512:4],
+                     T.PS[:, 32:64] if mn[j] == "V" else T.PS[:, 96:128] if "V" in mn else T.PS[:, 0:32], False, False, 32) for kk in range(4)],
+                   ["MX%d.%d" % (c, j), "PS", BK, BK + "x%d" % j], [BK + "m%d" % j], BK, group=(t, c))
+            KS = T.KS[:, 512 * c:512 * c + 512]
+            v(lambda KS=KS, bK=bK: V.tensor_tensor_scan(KS, T.RST[:], bK[:], 0.0, A.add, A.min),
+              ["RST", BK, BK + "w", BK + "e"] + [BK + "m%d" % j for j in range(4)], ["KS" + C], 512, [BK])
+            k0, p0, s0 = 512 * c, 40 * c, 32 * c
+            v(ts(T.PL[:, p0 + 8:p0 + 40], T.KS[:, k0 + 15:k0 + 512:16], 4095, None, A.bitwise_and), ["KS" + C], ["PL" + C], 32)
+            v(ts(T.PL[:, p0:p0 + 8], T.KS[:, k0 + 143:k0 + 256:16], 12, 15, A.arith_shift_right, A.bitwise_and), ["KS" + C], ["PK" + C], 8)
+            n_, f_, col_, pv_ = (T.PL[:, p0 + 8 * i:p0 + 8 * i + 8] for i in (1, 2, 3, 4))
+            if cfg["TO"][c]:
+                v(tt(T.TT[:, TT0 + 640:TT0 + 768], n_.indirect(T.BL[:, 0:8]), T.TT[:, TT0 + 128:TT0 + 256], A.is_equal),
+                  ["PL" + C, "BL", "TTe" + C], ["TTq" + C], gam * 128)
+                v(tt(T.TT[:, TT0 + 512:TT0 + 640], T.PL[:, p0:p0 + 8].indirect(T.BL[:, 0:8]), T.TT[:, TT0:TT0 + 128], A.is_equal),
+                  ["PK" + C, "BL", "TTk" + C], ["TTo" + C], gam * 128)
+            else:
+                v(tt(T.TT[:, TT0 + 512:TT0 + 768], T.PL[:, p0:p0 + 16].indirect(T.BL[:, 0:16]), T.TT[:, TT0:TT0 + 256], A.is_equal),
+                  ["PL" + C, "PK" + C, "BL", "TTk" + C, "TTe" + C], ["TTo" + C, "TTq" + C], gam * 256)
+            v(tt(T.T1[:, c8], n_, pv_, A.add), ["PL" + C], ["T1" + C], 16)
+            v(lambda c=c, TT0=TT0: V.tensor_tensor_scan(T.SS[:, 128 * c:128 * c + 128], T.KEEP[:], T.TT[:, TT0 + 640:TT0 + 768], 0.0,
+                                                        A.mult, A.add), ["KEEP", "TTq" + C], ["SS" + C], 128)
+            v(ts(T.T2[:, c8], T.T1[:, c8], 2047, None, A.bitwise_and), ["T1" + C], ["T2" + C], 8)
+            go, t4, dl, cw = (T.SM[:, s0 + 8 * i:s0 + 8 * i + 8] for i in range(4))
+            v(tt(dl, T.T2[:, c8], f_, A.subtract), ["T2" + C, "PL" + C], ["dl" + C], 16)
+            v(ts(go, T.SS[:, x0 + 15:x0 + 128:16], T.PAR[:], 6.0, A.subtract, A.is_ge), ["SS" + C, "PAR"], ["go" + C], 8)
+            v(ts(T.T3[:, c8], dl, 0.0, None, A.not_equal), ["dl" + C], ["T3" + C], 8)
+            v(tt(T.TT[:, TT0 + 256:TT0 + 384:16], n_, T.ZI[:, c8], A.subtract), ["PL" + C, "ZI" + C], ["TTd" + C], 16)
+            v(tt(t4, T.T3[:, c8], col_, A.mult), ["T3" + C, "PL" + C], ["T4" + C], 16)
+            v(tt(cw, t4, go, A.mult), ["T4" + C, "go" + C], ["cw" + C], 16)
+            o0 = 384 * c
+            mk = [["go" + C, "TTd" + C], ["PL" + C, "TTm" + C], ["dl" + C, "TTo" + C]]
+            for i, col in enumerate((go, col_, dl)):
+                o1, i1 = o0 + 128 * i, TT0 + 256 + 128 * i
+                if cfg["MO"][c][i] == "V":
+                    v(tt(T.MO[:, o1:o1 + 128], col.indirect(T.BL[:, 0:8]), T.TT[:, i1:i1 + 128], A.mult), mk[i] + ["BL"], ["MO%d.%d" % (c, i)],
+                      gam * 128)
+                else:
+                    def scaled(o1=o1, i1=i1, s1=s0 + 8 * i):
+                        r = None
+                        for q in range(8):
+                            r = S.activation(T.MO[:, o1 + 16 * q:o1 + 16 * q + 16], T.TT[:, i1 + 16 * q:i1 + 16 * q + 16], AF.Copy,
+                                             scale=T.SM[:, s1 + q:s1 + q + 1])
+                        return r
+                    op("A", scaled, mk[i], ["MO%d.%d" % (c, i)], 8 * 80)
+            M0, M1, M2 = ("MO%d.%d" % (c, i) for i in range(3))
+            Dm = T.MO[:, o0 + 128:o0 + 256]
+            BK = "bK" + C
+            mm([(bK[:, 0:256], T.ID[:], T.TRI[:], True, False, 256)], ["ID", "TRI0", "TRI1"], [BK], BK)
+            mm([(bK[:, 128 * h:128 * h + 128], T.BLK[:, 128 * h:128 * h + 128], Dm, False, h == 1, 128) for h in range(2)],
+               [M1, "BLK0", "BLK1"], [BK], BK)
+            mm([(bK[:, 376:384], T.ONE[0:1, :], T.C31[0:1, :], True, False, 8), (bK[:, 376:384], Dm, T.PS[:, 136:144], False, True, 8)],
+               [M1, "PS", "ONE", "C31"], [BK], BK)
+            if cfg["EQ"][c] == "V":
+                a(act(T.BM[:, 2 * x0:2 * x0 + 256], bK[:, 0:256], AF.Copy), [BK], ["BM" + C], 256, [BK])
+            else:
+                gather("A", T.BM[:, 2 * x0:2 * x0 + 256], cw.indirect(T.BL[:, 24:40]), ["cw" + C, "BL"], ["BM" + C], 256)
+            plus("LO", c, T.LO[:, c8], bK[:, 376:384], 0.0, [BK], ["LO" + C], 8, [BK])
+            gather("A", T.OLD[:, x0:x0 + 128], (T.F if c else T.F0)[:].indirect(T.LO[:, c8]), (FK if c else ["F0"]) + ["LO" + C], ["OLD" + C], 128)
+            mm([(T.bT[:, 0:128], T.REV[:], Wf, True, False, 128), (T.bT[:, 0:128], T.ZT[:, x0:x0 + 128], T.ID[:], False, False, 128),
+                (T.bT[:, 0:128], T.MO[:, o0:o0 + 128], T.ID[:], False, True, 128)], ["REV", WFk, "ZT" + C, M0, "ID"], ["bTa"], "bT")
+            mm([(T.bT[:, 128:256], T.MO[:, o0 + 256:o0 + 384], T.ID[:], True, False, 128),
+                (T.bT[:, 128:256], T.ID[:], T.OLD[:, x0:x0 + 128], False, True, 128)], [M2, "ID", "OLD" + C], ["bTb"], "bT")
+            if cfg["EQ"][c] == "V":
+                v(tt(T.EQ[:, 2 * x0:2 * x0 + 256], cw.indirect(T.BL[:, 24:40]), T.BM[:, 2 * x0:2 * x0 + 256], A.is_equal),
+                  ["cw" + C, "BL", "BM" + C], ["EQ" + C], gam * 256)
+            else:
+                v(tt(T.EQ[:, 2 * x0:2 * x0 + 256], bK[:, 0:256], T.BM[:, 2 * x0:2 * x0 + 256], A.is_equal), ["BM" + C, BK], ["EQ" + C], 256, [BK])
+            mm([(bK[:, 384:392], T.ONE[0:1, :], T.C31[0:1, :], True, False, 8), (bK[:, 384:392], Dm, T.PS[:, 136:144], False, False, 8)]
+               + [(bK[:, 384 + h:392:2], T.EQ[:, 2 * x0 + 128 * h:2 * x0 + 128 * h + 128], T.B32[:, 4 * h:4 * h + 4], False, h == 1, 4)
+                  for h in range(2)], ["EQ" + C, "B32", M1], [BK], BK)
+            if t < NV - 1:
+                w1 = w0 + 256
+                plus("SO", c, T.SO[:, w0:w0 + 128], T.bT[:, 0:128], 0.0, ["bTa"], ["SO%d%d" % (t, c)], 128, ["bT"])
+                a(act(T.SF[:, w0:w0 + 128], T.bT[:, 0:128], AF.Copy), ["bTa"], ["SF%d%d" % (t, c)], 128, ["bT"])
+                for k in "OF":
+                    arr = "arr%s%d%d" % (k, t + 1, c)
+                    op("G", lambda k=k, w0=w0, w1=w1, arr=arr: g.remote_dma(T["W" + k][:, w1:w1 + 128], T["S" + k][:, w0:w0 + 128], T.sem[arr],
+                                                                            T.sem.sent, pid, rid, mask),
+                       ["S%s%d%d" % (k, t, c)], ["W%s%d%d" % (k, t + 1, c)], 300, (), 2300, arr, -1)
+            else:
+                a(act(T.YW[:, x0:x0 + 128], T.bT[:, 0:128], AF.Copy), ["bTa"], ["YW" + C], 128, ["bT"])
+                dma("S", T.yw[:, x0:x0 + 128], T.YW[:, x0:x0 + 128], ["YW" + C], ["yw" + C], 2000)
+            a(act(T.DL[:, x0:x0 + 128], T.bT[:, 128:256], AF.Copy), ["bTb"], ["DL" + C], 128, ["bT"])
+            v(ts(T.LG[:, c8], bK[:, 384:392], T.NQ[:, 0:1], T.NQ[:, 1:2], A.max, A.min), [BK, "NQ0", "NQ1"], ["LG" + C], 8, [BK])
+            LGk = ["LG" + C]
+            if t < NV - 1:
+                op("P", lambda c=c, go=go: PE.matmul(T.bS[:, 144 + 8 * c:152 + 8 * c], T.ONEF[:], go, True, True),
+                   ["ONEF", "go" + C], ["bSa" + C], 256 * pe, ["bS"])
+            for j in range(3, -1, -1):
+                s = slice(x0 + 32 * j, x0 + 32 * j + 32)
+                v(cp(T.F[:].indirect(T.LG[:, 8 * c + 2 * j:8 * c + 2 * j + 2]), T.DL[:, s]), LGk + ["DL" + C], FK, sig * 32)
+        if t < NV - 1:
+            a(act(T.AJ[:], T.bS[:, 144:160], AF.Copy, accum_out=T.AS[:]), ["bSa0", "bSa1"], ["AS"], 40, ["bS"])
+            plus("Z1", 0, T.AI[:], T.AS[:], 0.0, ["AS"], ["AI"], 8)
+            v(ts(T.AP1[:], T.AI[:], 1, None, A.bitwise_and), ["AI"], ["AP1"], 8)
+            plus("ZT", 0, T.PAR[:], T.AP1[:], 0.0, ["AP1"], ["PAR"], 8)
+    now[0] = NV
+    for h, b in enumerate(("bR0", "bR1", "bM", "bK1")):
+        s = slice(256 * h, 256 * h + 256)
+        a(act(T[b][:, 0:256], T.F[:, FO + 1024 + 256 * h:FO + 1280 + 256 * h], AF.Identity, scale=2048.0), FK, [b], 256, [b])
+        v(tt(T.Y[:, s], T.F[:, FO + 256 * h:FO + 256 * h + 256], T[b][:, 0:256], A.add), FK + [b], ["Y%d" % (h // 2), "Yq%d" % h], 256, [b])
+        dma("S", T.yf[:, s], T.Y[:, s], ["Yq%d" % h], ["yf%d" % h], 2100)
+    return ops
+
+
+def arrange(ops, cfg):
+    n = len(ops)
+    lastw, readers = {}, {}
+    for i, o in enumerate(ops):
+        raw, other = set(), set()
+        for k in o["rd"]:
+            if k in lastw:
+                raw.add(lastw[k])
+        for k in o["wr"]:
+            if k in lastw:
+                other.add(lastw[k])
+            other.update(readers.get(k, ()))
+        other.discard(i)
+        o["raw"], o["dep"] = raw, raw | other
+        for k in o["rd"]:
+            readers.setdefault(k, set()).add(i)
+        for k in o["wr"]:
+            lastw[k] = i
+            readers[k] = set()
+    seen = {}
+    for o in ops:
+        k = ".".join(w[:2] + w[3] if w[:2] in ("SO", "SF", "WO", "WF") else w for w in (o["wr"][0], (o["rd"] + [""])[0]))
+        seen[k, o["t"]] = seen.get((k, o["t"]), 0) + 1
+        o["name"] = k + ("" if seen[k, o["t"]] == 1 else "#%d" % seen[k, o["t"]])
+    if cfg.get("places"):
+        cfg = dict(cfg, pos=dict(zip(sorted({o["name"] for o in ops}), [20 * int(x) for x in cfg["places"].split()])))
+    if cfg["pos"]:
+        return replay(ops, cfg)
+    wake = cfg["wake"]
+    succ = [[] for _ in range(n)]
+    for i, o in enumerate(ops):
+        for d in o["dep"]:
+            succ[d].append(i)
+    way = [0.0] * n
+    for i in range(n - 1, -1, -1):
+        way[i] = ops[i]["cost"] + ops[i]["lat"] + max([way[s] + wake for s in succ[i]] + [0.0])
+    seen = {}
+    for i, o in enumerate(ops):
+        way[i] = cfg["look"] * way[i]
+    left = [len(o["dep"]) for o in ops]
+    ready = [i for i in range(n) if left[i] == 0]
+    free, end, bank = {}, [0.0] * n, {}
+    order = []
+
+    def waits(i, d):
+        o, p = ops[i], ops[d]
+        return p["q"] != o["q"] or p["sem"] is not None or (o["q"] != "P" and (d in o["raw"] or cfg["same"]))
+
+    while ready:
+        best = None
+        for i in ready:
+            o = ops[i]
+            st = free.get(o["q"], 0.0)
+            for d in o["dep"]:
+                if waits(i, d):
+                    st = max(st, end[d] + wake)
+            for b in o["banks"]:
+                for (q, d) in bank.get(b, {}).items():
+                    if q != o["q"]:
+                        st = max(st, end[d] + wake)
+            key = (st - way[i], i)
+            if best is None or key < best[0]:
+                best = (key, i, st)
+        _, i, st = best
+        o = ops[i]
+        for b in o["banks"]:
+            for (q, d) in bank.setdefault(b, {}).items():
+                if q != o["q"]:
+                    o["dep"].add(d)
+            bank[b][o["q"]] = i
+        o["wait"] = [d for d in o["dep"] if waits(i, d)]
+        o["start"] = st
+        free[o["q"]] = st + o["cost"]
+        end[i] = st + o["cost"] + o["lat"]
+        order.append(i)
+        ready.remove(i)
+        for s in succ[i]:
+            left[s] -= 1
+            if left[s] == 0:
+                ready.append(s)
+    return order, max(end)
+
+
+def replay(ops, cfg):
+    n = len(ops)
+    key = [-1e6 if o["t"] < 0 and o["sem"] else max(o["t"], 0) * 20000 + cfg["pos"][o["name"]] for o in ops]
+    succ = [[] for _ in range(n)]
+    for i, o in enumerate(ops):
+        for d in o["dep"]:
+            succ[d].append(i)
+    left = [len(o["dep"]) for o in ops]
+    ready = [i for i in range(n) if left[i] == 0]
+    free, end, bank, order = {}, [0.0] * n, {}, []
+    while ready:
+        i = min(ready, key=lambda j: (key[j], j))
+        ready.remove(i)
+        o = ops[i]
+        for b in o["banks"]:
+            for (q, d) in bank.setdefault(b, {}).items():
+                if q != o["q"]:
+                    o["dep"].add(d)
+            bank[b][o["q"]] = i
+        o["wait"] = [d for d in o["dep"] if ops[d]["q"] != o["q"] or ops[d]["sem"] is not None or o["q"] != "P"]
+        o["start"] = max([free.get(o["q"], 0.0)] + [end[d] + cfg["wake"] for d in o["wait"]])
+        free[o["q"]] = o["start"] + o["cost"]
+        end[i] = free[o["q"]] + o["lat"]
+        order.append(i)
+        for s in succ[i]:
+            left[s] -= 1
+            if left[s] == 0:
+                ready.append(s)
+    return order, max(end)
+
+
+def rank_program(g, core, T, topo):
+    rank = T.rank_of(core)
+    if rank is None:
+        return
+    ops = build(g, T, topo, core, CFG)
+    order, _ = arrange(ops, dict(CFG, places=PLACES))
+    queue = {"V": g.vector, "A": g.scalar, "P": g.tensor, "G": g, "S": g.sync}
+    pos = {i: p for p, i in enumerate(order)}
+    known = {q: {} for q in queue}
+    plan, signal = {}, set()
+    for i in order:
+        o = ops[i]
+        kn = known[o["q"]]
+        need = []
+        for d in sorted(o["wait"], key=lambda d: -pos[d]):
+            p = ops[d]
+            key = p["sem"] or p["q"]
+            if kn.get(key, -1) >= pos[d]:
+                continue
+            need.append(d)
+            signal.add(d)
+            if p["cnt"] >= 0:
+                for k, val in p["known"].items():
+                    kn[k] = max(kn.get(k, -1), val)
+            kn[key] = pos[d]
+        o["known"] = dict(kn)
+        plan[i] = need
+    last = {}
+    for i in order:
+        if ops[i].get("group"):
+            last[ops[i]["group"]] = i
+    for i in last.values():
+        ops[i]["close"][0] = True
+    count, total = {}, {}
+    sent = 0
+    for i in order:
+        o = ops[i]
+        for d in plan[i]:
+            queue[o["q"]].wait_ge(T.sem[ops[d]["sem"] or "c" + ops[d]["q"]], count[d])
+        r = o["fn"]()
+        if o["sem"] is None:
+            if i in signal:
+                total["c" + o["q"]] = count[i] = total.get("c" + o["q"], 0) + 1
+                r.then_inc(T.sem["c" + o["q"]], 1)
+        else:
+            if o["cnt"] > 0:
+                total[o["sem"]] = count[i] = o["cnt"]
+                r.then_inc(T.sem[o["sem"]], o["cnt"])
+            else:
+                total[o["sem"]] = count[i] = len(topo.engines(T.cores[rank - 1], core))
+                sent += len(topo.engines(core, T.cores[(rank + 1) % len(T.cores)]))
+    total["sent"] = sent
+    for s, c in total.items():
+        g.wait_ge(T.sem[s], c)

@@ -2,58 +2,57 @@ from concourse.mybir import AluOpType as A, ActivationFunctionType as AF
 
 NV = 4
 FO = 32
-MAGIC = 1.5 * 2.0 ** 34
+MAGIC = 1.5 * 2.0 ** 24
+QV, QZ, QK, QC, QS, Q1, Q2 = range(7)
 
 SCRATCH = {
     "fin": ("sbuf", [128, 1024], "int32"), "wi": ("sbuf", [128, 256], "int32"),
-    "Y": ("sbuf", [128, 1024], "float32"), "F": ("sbuf", [128, FO + 2064], "int32"),
-    "rec2": ("sbuf", [128, 4096], "bfloat16"),
+    "Y": ("sbuf", [128, 1024], "float32"), "F": ("sbuf", [128, FO + 2064], "int32"), "R": ("sbuf", [128, 4096], "bfloat16"),
     "G": ("sbuf", [128, 4096], "float16"), "X": ("sbuf", [128, 4096], "bfloat16"), "MX": ("sbuf", [128, 4096], "bfloat16"),
-    "WO": ("sbuf", [128, 256 * NV], "uint16"), "WF": ("sbuf", [128, 256 * NV], "float16"),
-    "SO": ("sbuf", [128, 256 * NV], "uint16"), "SF": ("sbuf", [128, 256 * NV], "float16"),
-    "YW": ("sbuf", [128, 256], "float32"),
+    "WO": ("sbuf", [128, 256 * NV], "uint16"), "WF": ("sbuf", [128, 256 * NV], "float16"), "SF": ("sbuf", [128, 256 * NV], "float16"),
+    "YW": ("sbuf", [128, 256], "float32"), "F0": ("sbuf", [128, FO + 2064], "int32"),
     "EO": ("sbuf", [128, 256], "uint16"), "VT": ("sbuf", [128, 256], "float16"), "NG": ("sbuf", [128, 256], "bfloat16"),
-    "TT": ("sbuf", [128, 1536], "float16"), "MO": ("sbuf", [128, 768], "float16"),
-    "MB": ("sbuf", [128, 256], "bfloat16"), "KS": ("sbuf", [128, 1024], "int32"), "SS": ("sbuf", [128, 256], "float32"),
-    "PL": ("sbuf", [128, 80], "int32"), "SM": ("sbuf", [128, 64], "float32"),
-    "T1": ("sbuf", [128, 16], "int32"), "T2": ("sbuf", [128, 16], "int32"), "T3": ("sbuf", [128, 16], "float32"),
-    "T4": ("sbuf", [128, 16], "float32"),
-    "U2": ("sbuf", [128, 16], "float32"), "Z1": ("sbuf", [128, 16], "int32"), "ZI": ("sbuf", [128, 16], "int32"),
-    "ZT": ("sbuf", [128, 256], "float16"), "BM": ("sbuf", [128, 512], "float32"), "EQ": ("sbuf", [128, 512], "bfloat16"),
-    "LG": ("sbuf", [128, 16], "uint16"),
-    "OLD": ("sbuf", [128, 256], "float16"), "DL": ("sbuf", [128, 256], "int32"),
-    "AJ": ("sbuf", [128, 16], "float32"), "AS": ("sbuf", [128, 1], "float32"), "AI": ("sbuf", [128, 1], "int32"),
-    "AP1": ("sbuf", [128, 1], "int32"), "PAR": ("sbuf", [128, 1], "float32"),
-    "ONE": ("sbuf", [128, 128], "bfloat16"), "NONE": ("sbuf", [128, 128], "bfloat16"), "ONEF": ("sbuf", [128, 128], "float32"),
-    "ID": ("sbuf", [128, 128], "bfloat16"), "NID": ("sbuf", [128, 128], "bfloat16"),
-    "ODD": ("sbuf", [128, 128], "bfloat16"), "NODD": ("sbuf", [128, 128], "bfloat16"),
-    "SH": ("sbuf", [128, 128], "bfloat16"), "NSH": ("sbuf", [128, 128], "bfloat16"),
-    "KEEP": ("sbuf", [128, 128], "bfloat16"), "SHF": ("sbuf", [128, 128], "bfloat16"), "REV": ("sbuf", [128, 128], "bfloat16"),
-    "DR": ("sbuf", [128, 128], "bfloat16"), "BL0": ("sbuf", [128, 256], "bfloat16"), "BLK": ("sbuf", [128, 256], "bfloat16"),
-    "PS0": ("sbuf", [128, 144], "bfloat16"), "PS1": ("sbuf", [128, 144], "bfloat16"), "PS": ("sbuf", [128, 144], "bfloat16"),
-    "IK": ("sbuf", [128, 128], "bfloat16"), "KC": ("sbuf", [128, 512], "bfloat16"), "N192": ("sbuf", [128, 512], "bfloat16"),
-    "RST": ("sbuf", [128, 512], "bfloat16"), "TRI": ("sbuf", [128, 256], "bfloat16"), "WT": ("sbuf", [128, 8], "bfloat16"),
-    "PI": ("sbuf", [128, 1], "int32"), "PI2": ("sbuf", [128, 2], "int32"), "PLO": ("sbuf", [128, 1], "float32"),
-    "NQ": ("sbuf", [128, 2], "float32"), "W2": ("sbuf", [128, 1], "float32"), "PQ": ("sbuf", [128, 2], "float32"),
-    "BLI": ("sbuf", [128, 40], "int32"), "BL": ("sbuf", [128, 40], "uint16"),
-    "B31": ("sbuf", [128, 8], "bfloat16"), "B32": ("sbuf", [128, 8], "bfloat16"), "F0": ("sbuf", [128, FO + 2064], "int32"),
-    "B30": ("sbuf", [128, 8], "bfloat16"), "C31": ("sbuf", [128, 8], "bfloat16"), "LO": ("sbuf", [128, 16], "uint16"),
-    "bK0": ("psum", [128, 512], "float32"), "bK1": ("psum", [128, 512], "float32"), "bM": ("psum", [128, 512], "float32"),
-    "bR0": ("psum", [128, 512], "float32"), "bR1": ("psum", [128, 512], "float32"), "bV": ("psum", [128, 512], "float32"),
-    "bS": ("psum", [128, 512], "float32"), "bT": ("psum", [128, 512], "float32"),
+    "MB": ("sbuf", [128, 256], "bfloat16"), "KS": ("sbuf", [128, 1024], "int32"), "KP": ("sbuf", [128, 256], "float32"),
+    "PL": ("sbuf", [128, 96], "int32"), "U2": ("sbuf", [128, 16], "float32"),
+    "QW": ("sbuf", [128, 128], "float16"), "QT": ("sbuf", [128, 256], "float16"),
+    "DM": ("sbuf", [128, 256], "float16"), "EV": ("sbuf", [128, 256], "bfloat16"), "SS": ("sbuf", [128, 256], "bfloat16"),
+    "PR": ("sbuf", [128, 256], "float16"), "EQ": ("sbuf", [128, 512], "bfloat16"),
+    "TT": ("sbuf", [128, 512], "float16"), "BS": ("sbuf", [128, 512], "float32"), "SM": ("sbuf", [128, 64], "float32"),
+    "LO": ("sbuf", [128, 16], "uint16"), "LG": ("sbuf", [128, 16], "uint16"),
+    "OLD": ("sbuf", [128, 256], "float16"), "CL": ("sbuf", [128, 256], "float32"), "DL": ("sbuf", [128, 256], "int32"),
+    "AC": ("sbuf", [128, 2], "float32"), "AR": ("sbuf", [128, 1], "float32"), "NP": ("sbuf", [128, 1], "float32"),
+    "ONE": ("sbuf", [128, 128], "bfloat16"), "ODD": ("sbuf", [128, 128], "bfloat16"), "OFF": ("sbuf", [128, 128], "bfloat16"),
+    "IK": ("sbuf", [128, 256], "bfloat16"), "BI": ("sbuf", [128, 16], "int32"), "BL": ("sbuf", [128, 16], "uint16"),
+    "PI": ("sbuf", [128, 4], "int32"), "PF": ("sbuf", [128, 16], "float32"),
+    "GM0": ("sbuf", [128, 16], "bfloat16"), "GM": ("sbuf", [128, 16], "bfloat16"), "GB": ("sbuf", [128, 8], "bfloat16"),
+    "ROW": ("sbuf", [128, 912], "bfloat16"), "IDS": ("sbuf", [128, 256], "bfloat16"), "NID": ("sbuf", [128, 128], "bfloat16"),
+    "CF": ("sbuf", [128, 128], "float32"), "NSH": ("sbuf", [128, 128], "bfloat16"),
+    "SHF": ("sbuf", [128, 128], "bfloat16"), "REV": ("sbuf", [128, 128], "bfloat16"), "KEEP": ("sbuf", [128, 128], "bfloat16"),
+    "DR": ("sbuf", [128, 128], "bfloat16"), "MK": ("sbuf", [128, 128], "bfloat16"),
+    "BK0": ("sbuf", [128, 256], "bfloat16"), "BLK": ("sbuf", [128, 256], "bfloat16"),
+    "TR0": ("sbuf", [128, 256], "bfloat16"), "TRI": ("sbuf", [128, 256], "bfloat16"),
+    "PS": ("sbuf", [128, 96], "bfloat16"), "WT": ("sbuf", [128, 8], "bfloat16"),
+    "B30": ("sbuf", [128, 8], "bfloat16"), "B31": ("sbuf", [128, 8], "bfloat16"), "B32": ("sbuf", [128, 8], "bfloat16"),
+    "RST": ("sbuf", [128, 256], "bfloat16"), "CT": ("sbuf", [128, 192], "bfloat16"), "CQ": ("sbuf", [128, 512], "bfloat16"),
+    "RL": ("sbuf", [128, 512], "float16"),
 }
-SEMAPHORES = (["cV", "cA", "cP", "cG", "sent"] + ["arr%s%d%d" % (k, t, c) for k in "OF" for t in range(1, NV) for c in range(2)]
+for _b in "KPMQ":
+    for _c in "01":
+        SCRATCH["b" + _b + _c] = ("psum", [128, 512], "float32")
+SEMAPHORES = (["cV", "cA", "cP", "cG", "sent"] + ["arr%d%d" % (t, c) for t in range(1, NV) for c in range(2)]
               + ["dma%d" % i for i in range(15)])
 
 CFG = {
-    "pos": {}, "FG": {1: "AAAAVVVV", 0: "AA AA VV VV"}, "XG": {1: "AA AA VV VV", 0: "AA AA AA AA"}, "MN": {1: "VVVV", 0: "VAVA"},
-    "MO": {1: "VVV", 0: "VVV"}, "EQ": {1: "V", 0: "V"},
-    "Z1": {1: "A", 0: "A"}, "ZT": {1: "A", 0: "A"}, "LO": {1: "A", 0: "A"}, "SO": {1: "A", 0: "A"}, "EO": {1: "V", 0: "V"},
-    "TO": {1: 0, 0: 1}, "VS": {1: 4, 0: 1}, "VE": {1: "V", 0: "A"},
-    "gam": 1.56, "sig": 3.5, "pe": 0.45, "wake": 70.0, "same": True, "look": 0.02, "seed": 0, "noise": 0.0,
+    "FG": {1: "AAAA VVVV", 0: "AAAA VVVV"}, "XG": {1: "AA AA VV VV", 0: "AA AA AA VV"}, "MN": {1: "VVVV", 0: "AAAA"},
+    "VS": {1: 1, 0: 1}, "HS": {1: 1, 0: 1}, "RD": 1, "NB": 3, "F0": 1, "KI": 384, "EQ": "VV", "DL": "VV",
+    "WO": "VV", "VT": "AA", "EO": "VV", "QW": "VV", "QT": "AA", "LO": "AA", "OLD": "AA", "SF": "AA", "TT": "AA", "BS": "AA",
+    "gam": 1.56, "sig": 3.8, "pe": 0.42, "wake": 70.0, "far": 2600.0, "far0": 2000.0, "least": 8, "visit": "", "first": "",
 }
-CFG.update({'FG': {1: 'AA AA VVVV', 0: 'AA AAAVVV'}, 'XG': {1: 'A V AA VAVV', 0: 'VA AV AAA V'}, 'MN': {1: 'VVVV', 0: 'AAAA'}, 'MO': {1: 'VVA', 0: 'VVA'}, 'EQ': {1: 'A', 0: 'V'}, 'TO': {1: 0, 0: 0}, 'VS': {1: 4, 0: 1}, 'VE': {1: 'V', 0: 'A'}})
-PLACES = """1235 1444 1219 28 5 344 126 787 246 317 299 367 333 388 998 913 106 1095 999 352 497 425 1065 985 239 50 996 1092 1254 1057 1038 1048 1093 1062 -54 158 177 220 230 414 394 390 178 338 353 33 136 54 52 871 758 1116 1020 944 908 697 566 1032 967 881 886 884 883 860 728 769 853 657 727 597 596 -31 502 422 321 -3 12 733 813 -42 68 1044 957 -17 1002 29 1625 268 474 441 929 807 917 766 500 750 589 312 49 103 138 -122 70 -138 16 -139 215 17 308 113 292 1236 909 30 96 1091 956 988 866 952 803 968 822 989 863 1031 885 879 732 1006 823 618 530 421 738 763 848 955 859 876 751 442 345 588 1076 912 112 1124 1001 120 656 513 565 585 590 610 514 436 473 521 456 439 451 260 145 90 141 1201 962 889 705 931 689 8 963 717 1105 954 1015 970 200 887 888 851 882 875 393 1021 283 902 838 904 247 579 672 663 592 595 302 531 529 594 593 135 768 581 27 796 170 325 839 396 806 318 391 245 212 281 707 256 789 587 501 643 518 1139 1148 868 601 910 924 1047 987 759 458 364 673 586 447 1045 890 981 858 -9 -62 1007 880 53 51 -41 250 243 275 242 1159 965"""
+
+
+CFG.update({'FG': {1: 'VV AAAA V V', 0: 'AAAAA V V V'}, 'XG': {1: 'VV AA A VVV', 0: 'V V V A A A V A'}, 'MN': {1: 'VVVV', 0: 'AAAA'}, 'VS': {1: 1, 0: 1}, 'HS': {1: 1, 0: 1}, 'RD': 1, 'NB': 3, 'F0': 1, 'KI': 128, 'EQ': 'AV', 'DL': 'AV', 'WO': 'AV', 'VT': 'VA', 'EO': 'VA', 'QW': 'VA', 'QT': 'AA', 'LO': 'VV', 'OLD': 'VA', 'SF': 'AA', 'TT': 'AA', 'BS': 'AA'})
+CFG["visit"] = 'AG1.2 VG1.0 VG1.6 keep mprev0 VWO0 mkw0 VG1.7 mkey1 AG0.0 VG0.7 mpick1 VG0.5 VVT1 VG0.6 mturn1 mtd0 mn1921 VEO1 mkw1 VNG1 AX1.2 VX1.0 mtt1 mpick0 VX1.5 ATT1 msum1.0 AVT0 AX1.4 mturn0 mke1 AEO0 VAR+ VNG0 msum1.1 AX0.7 VX0.0 VX0.1 AX0.3 mkx1.3 mtt0 VX0.2 mkx1.0 AMB1.0 mkx1.2 AX0.4 mkx1.1 VX0.6 mwide1.0 AX0.5 msum0.0 VMX1.0.0 ATT0 msum0.1 VMX1.2.0 mx0.1.0 VNP+ VMX1.3.0 AMB0.0 mu1 mkm1.0 mx0.0.0 AU21 VMX1.1.0 AKZ1 mkm1.2 msub0.0.0 mkm1.3 mkm1.1 AMX0.0.0 msub0.1.0 VKS1 mx0.2.0 VKP1 AMX0.1.0 msub0.2.0 VPL1 VPK1 VT11 VEV1 mx0.3.0 AQS1 VPC1 AMX0.2.0 msub0.3.0 VDM1 VSS1 mkm0.1 VPV1 mlo1 VGO1 AMX0.3.0 VQW1 mkm0.2 VTD1 mq1 VPR1 mke0 mkm0.0 AQT1 VLO1 VCW1 mkm0.3 VOLD1 ABW1 mwin1 mnew1 VKS0 mu0 mtri1 mover1 ASF1 VKP0 AU20 VPL0 VPK0 mblk1 send1 VT10 VDM0 AKZ0 ARL1 VPV0 VPC0 mlo0 VEV0 AQS0 mlist0 AAC1 mmend1 AQW0 VEQ1 mlist1 mq0 VSS0 ADL1 VLO0 mvoid1 VTD0 mtri0 AQT0 VGO0 mblk0 VLG1 AOLD0 VPR0 mbound0 AAC0 mwin0 Vput7 ABS0 mnew0 VCW0 VCL0 Vput6 ASF0 VEQ0 send0 Vput5 mvoid0 VDL0 mkey0- Vput4 VLG0 AWO1- mtd1- Vput3 mprev1- mback Vput2 Vput1 Vput0'
+CFG["first"] = 'swi afin0 sfin1 srec srec2 gPI vONE vB300 vKC0 gGM0 vPI0 vPI1 gID vPF vNP vRST ar1 ar2 gGM vQW0 aw2 vCT aNID gODD vFe vB301 aPS1b vCF aGB vKC aCTs vC32 arow0 gSH vN192 aPS0b aCTv aCTk aPS0a aCTz gB31 aCTr aCTo gIK aNSH aCTn aWF01 vWO01 mct gKEEP vFd vRST#2 @mkey0 aFh0 vFl0 gSHF @mtd1 aFh1 vFl1 gBI gREV vTR0 aWT aCQ gOFF @AG1.2 gBK01 vDR gB32 @VG1.6 gBK00 @keep gBLK0 @mkey1 gBLK1 @mpick1 vTRI @VVT1 vBL @msum1.1 alow @mkx1.2 aPS1a @msum0.1 ahigh @mx0.0.0 vMK @mkm1.3'
 
 
 def parts(text):
@@ -74,20 +73,20 @@ def build(g, T, topo, core, cfg):
     gam, sig, pe = cfg["gam"], cfg["sig"], cfg["pe"]
     ndma, now = [0], [-1]
 
-    def op(q, fn, rd, wr, cost, banks=(), lat=0.0, sem=None, cnt=0):
+    def op(q, fn, rd, wr, cost, banks=(), lat=0.0, sem=None, cnt=0, name=None):
         ops.append({"q": q, "fn": fn, "rd": list(rd), "wr": list(wr), "cost": cost, "banks": list(banks), "lat": lat,
-                    "sem": sem, "cnt": cnt, "t": now[0]})
+                    "sem": sem, "cnt": cnt, "t": now[0], "name": name})
+
+    def call(name):
+        ops[-1]["name"] = name
 
     def v(fn, rd, wr, n, banks=()):
-        op("V", fn, rd, wr, 50 + 0.83 * n, banks)
+        op("V", fn, rd, wr, 50 + 0.83 * max(n, cfg["least"]), banks)
 
     def a(fn, rd, wr, n, banks=()):
-        op("A", fn, rd, wr, 65 + 0.83 * n, banks)
+        op("A", fn, rd, wr, 65 + 0.83 * max(n, cfg["least"]), banks)
 
-    def gp(fn, rd, wr, n):
-        op("G", fn, rd, wr, 170 + 1.66 * n)
-
-    def mm(lst, rd, wr, bank, least=64, group=None):
+    def mm(name, lst, rd, wr, bank, least=64, group=None):
         close = [False]
 
         def fn():
@@ -95,7 +94,8 @@ def build(g, T, topo, core, cfg):
             for i, (o, l, rh, st, sp, n) in enumerate(lst):
                 r = PE.matmul(o, l, rh, st, sp or (close[0] and i == len(lst) - 1))
             return r
-        op("P", fn, rd, wr, sum(max(least, m[5]) * pe + 5 for m in lst), [bank])
+        op("P", fn, rd, list(wr) + ([] if group else ["order " + bank]), sum(max(least, m[5]) * pe + 3 for m in lst), [bank], 60.0,
+           name="m" + name)
         ops[-1]["group"], ops[-1]["close"] = group, close
 
     def dma(q, out, in_, rd, wr, lat):
@@ -120,70 +120,114 @@ def build(g, T, topo, core, cfg):
     def act(o, i, f, **kw):
         return lambda: S.activation(o, i, f, **kw)
 
-    def sel(o, i, pat, cmp, base, cm):
-        return lambda: g.affine_select(o, i, pat, cmp, 0.0, base, cm)
+    def scan(o, d0, d1, o0, o1):
+        return lambda: V.tensor_tensor_scan(o, d0, d1, 0.0, o0, o1)
 
-    def iota(o, pat, base, cm, flag=True):
+    def iota(o, key, pat, cm, n, flag=True):
         if flag:
-            return lambda: g.iota(o, pat, base, cm, allow_small_or_imprecise_dtypes=True)
-        return lambda: g.iota(o, pat, base, cm)
+            op("G", lambda: g.iota(o, pat, 0, cm, allow_small_or_imprecise_dtypes=True), [], [key], 130 + 1.66 * n)
+        else:
+            op("G", lambda: g.iota(o, pat, 0, cm), [], [key], 130 + 1.66 * n)
 
-    dma("S", T.wi[:], T.wnd[:], [], ["wi", "q0"], 2000)
-    dma("A", T.fin[:, 0:512], T.fld[:, 0:512], [], ["fin0"], 2500)
-    dma("S", T.fin[:, 512:1024], T.fld[:, 512:1024], [], ["fin1"], 3000)
-    dma("S", T.rec2[:, 0:2048], T.rec[:], [], ["rec0"], 4200)
-    dma("S", T.rec2[:, 2048:4096], T.rec[:], [], ["rec1"], 5400)
+    def sel(o, key, i, rd, pat, cmp, base, cm, n=128, fill=0.0):
+        op("G", lambda: g.affine_select(o, i, pat, cmp, fill, base, cm), rd, [key], 170 + 1.66 * n)
+
+    def plus(who, out, in_, add, rd, wr, n, banks=(), half=False):
+        if who == "A":
+            a(act(out, in_, AF.Identity, bias=add) if add else act(out, in_, AF.Copy), rd, wr, n, banks)
+        else:
+            v(ts(out, in_, add, None, A.add) if add else cp(out, in_), rd, wr, n / 2 if half else n, banks)
+
+    def gather(who, out, win, rd, wr, n):
+        if who == "V":
+            v(cp(out, win), rd, wr, gam * n)
+        else:
+            a(act(out, win, AF.Copy), rd, wr, gam * n)
+
+    dma("S", T.wi[:], T.wnd[:], [], ["wi"], 2200)
+    dma("A", T.fin[:, 0:512], T.fld[:, 0:512], [], ["fin0"], 2700)
+    dma("S", T.fin[:, 512:1024], T.fld[:, 512:1024], [], ["fin1"], 3200)
+    dma("S", T.R[:, 0:2048], T.rec[:], [], ["rec"], 4400)
+    if cfg["RD"]:
+        dma("S", T.R[:, 2048:4096], T.rec[:], [], ["rec2"], 5600)
+    ID, SH, ONE = T.IDS[:, 128:256], T.IDS[:, 0:128], T.ONE[0:1, :]
+    N192, KC, C32 = T.ROW[0:1, 0:512], T.ROW[0:1, 512:896], T.ROW[0:1, 896:904]
     v(ms(T.ONE[:], 1.0), [], ["ONE"], 64)
-    v(ms(T.NONE[:], -1.0), [], ["NONE"], 64)
-    v(ms(T.ONEF[:], 1.0), [], ["ONEF"], 128)
+    for key, lo, hi, val in (("N192", 0, 512, -192.0), ("KC0", 512, 768, 0.0), ("KC", 768, 896, -65536.0), ("C32", 896, 912, FO + 0.0)):
+        v(ms(T.ROW[0:32, lo:hi], val), [], [key], (hi - lo) / 2)
     v(ms(T.F[:, 0:FO], 0), [], ["Fd"], 32)
-    v(ms(T.PAR[:], 0.0), [], ["PAR"], 8)
-    v(ms(T.N192[:], -192.0), [], ["N192"], 256)
-    v(ms(T.ZT[:], 0.0), [], ["ZT0", "ZT1"], 128)
-    for i, (lo, hi, val) in enumerate([(0, 8, 1.0), (8, 32, -1.0), (32, 40, -2.0), (40, 64, 2.0), (64, 72, -1.0), (72, 96, 1.0),
-                                       (96, 104, 2.0), (104, 128, -2.0), (128, 136, -1.0 / 16), (136, 144, 2.0 ** -16)]):
-        v(ms(T.PS0[:, lo:hi], val * 65536.0), [], ["PS0.%d" % i], 8)
-    gp(sel(T.ID[:], T.ONE[:], [[-1, 128]], A.is_equal, 0, 1), ["ONE"], ["ID"], 128)
-    gp(iota(T.NODD[:], [[0, 64], [-1, 2]], 0, 0), [], ["NODD"], 128)
-    gp(sel(T.NSH[:], T.NODD[:], [[-1, 128]], A.is_equal, 1, 1), ["NODD"], ["NSH"], 128)
-    gp(iota(T.IK[:], [[0, 8], [1, 16]], 0, 0), [], ["IK"], 128)
-    gp(iota(T.PI[:], [[0, 1]], 0, 1, False), [], ["PI"], 1)
-    gp(iota(T.BLI[:, 0:24], [[1, 24]], 0, 0, False), [], ["BLI"], 24)
-    gp(iota(T.KC[:], [[0, 32], [4096, 16]], 0, 0), [], ["KC"], 512)
-    gp(sel(T.NID[:], T.NONE[:], [[-1, 128]], A.is_equal, 0, 1), ["NONE"], ["NID"], 128)
-    gp(sel(T.KEEP[:], T.ONE[:], [[0, 8], [1, 16]], A.is_gt, 0, 0), ["ONE"], ["KEEP"], 128)
-    gp(sel(T.SHF[:], T.KEEP[:], [[-1, 128]], A.is_equal, 1, 1), ["KEEP"], ["SHF"], 128)
-    gp(sel(T.REV[:], T.KEEP[:], [[-16, 8], [1, 16]], A.is_equal, -15, 1), ["KEEP"], ["REV"], 128)
-    gp(sel(T.PS1[:], T.PS0[:], [[0, 18], [-16, 8]], A.is_ge, 0, 1), ["PS0.%d" % i for i in range(10)], ["PS1"], 144)
-    gp(sel(T.PS[:], T.PS1[:], [[0, 18], [16, 8]], A.is_ge, 15, -1), ["PS1"], ["PS"], 144)
-    v(ts(T.ODD[:], T.ID[:], -1.0, 1.0, A.mult, A.add), ["ID"], ["ODD"], 64)
-    v(ms(T.C31[:], FO - 1.0), [], ["C31"], 8)
-    v(ms(T.B30[:, 0:4], -4096.0), [], ["B30a"], 8)
-    v(ms(T.B30[:, 4:8], 4096.0), [], ["B30b"], 8)
-    v(ms(T.F[:, FO + 2048:FO + 2064], 0), [], ["Fe"], 8)
+    v(ms(T.F[:, FO + 2048:FO + 2064], 0), [], ["Fe"], 16)
+    v(ms(T.NP[:], 0.0), [], ["NP"], 8)
+    v(ms(T.CF[:], 1.0), [], ["CF"], 128)
+    v(ms(T.CT[:], 0.0), [], ["CT"], 96)
+    v(ms(T.RST[:], 2048.0), [], ["RST"], 128)
+    v(ms(T.RST[:, 0:256:16], -2.0 ** 26), [], ["RST"], 16)
+    v(ms(T.QW[:], 1.0), [], ["QW0", "QW1", "QS0", "QS1"], 64)
+    for h in range(2):
+        v(ms(T.B30[:, 4 * h:4 * h + 4], 8192.0 * h - 4096.0), [], ["B30%d" % h], 8)
+    iota(T.PI[:, 0:1], "PI", [[0, 1]], 1, 1, False)
+    sel(ID, "ID", T.ONE[:], ["ONE"], [[-1, 128]], A.is_equal, 0, 1)
+    iota(T.ODD[:], "ODD", [[0, 64], [1, 2]], 0, 128)
+    sel(SH, "SH", T.ODD[:], ["ODD"], [[-1, 128]], A.is_equal, 1, 1)
+    sel(T.GM0[:], "GM0", T.ONE[:, 0:16], ["ONE"], [[0, 2], [-16, 8]], A.is_ge, 0, 1, 16)
+    sel(T.GM[:], "GM", T.GM0[:], ["GM0"], [[0, 2], [16, 8]], A.is_ge, 15, -1, 16)
+    iota(T.IK[:], "IK", [[16, 2], [0, 8], [1, 16]], 0, 256)
+    iota(T.BI[:], "BI", [[0, 2], [1, 8]], 0, 16, False)
+    sel(T.KEEP[:], "KEEP", T.ONE[:], ["ONE"], [[0, 8], [1, 16]], A.is_gt, 0, 0)
+    sel(T.SHF[:], "SHF", T.KEEP[:], ["KEEP"], [[-1, 128]], A.is_equal, 1, 1)
+    sel(T.REV[:], "REV", T.KEEP[:], ["KEEP"], [[-16, 8], [1, 16]], A.is_equal, -15, 1)
+    sel(T.OFF[:], "OFF", T.ONE[:], ["ONE"], [[-1, 128]], A.not_equal, 0, 1)
     for h in range(2):
         s = slice(128 * h, 128 * h + 128)
-        gp(sel(T.BL0[:, s], T.ODD[:], [[-32, 4], [0, 32]], A.is_ge, -16 * h, 1), ["ODD"], ["BL0%d" % h], 128)
-        gp(sel(T.BLK[:, s], T.BL0[:, s], [[32, 4], [0, 32]], A.is_ge, 16 * h + 15, -1), ["BL0%d" % h], ["BLK%d" % h], 128)
-    gp(sel(T.B31[:], T.B30[:], [[0, 2], [-32, 4]], A.is_ge, 0, 1), ["B30a", "B30b"], ["B31"], 8)
-    gp(sel(T.B32[:], T.B31[:], [[0, 2], [32, 4]], A.is_ge, 31, -1), ["B31"], ["B32"], 8)
-    v(ts(T.SH[:], T.NSH[:], -1.0, None, A.mult), ["NSH"], ["SH"], 64)
-    v(ts(T.PI2[:, 0:1], T.PI[:], 15, None, A.bitwise_and), ["PI"], ["PI2"], 8)
-    v(ts(T.PI2[:, 1:2], T.PI[:], 31, None, A.bitwise_and), ["PI"], ["PI3"], 8)
-    v(cp(T.PLO[:], T.PI2[:, 0:1]), ["PI2"], ["PLO"], 8)
-    v(ts(T.W2[:], T.PLO[:], 2.0, 1.0, A.mult, A.add), ["PLO"], ["W2"], 8)
-    v(ts(T.WT[:], T.PS[:, 136:144], T.W2[:], None, A.mult), ["PS", "W2"], ["WT"], 8)
-    for h in range(2):
-        v(ts(T.NQ[:, h:h + 1], T.PLO[:], 2.0 * h - 1, FO - 1.0 + 2049 * h, A.mult, A.add), ["PLO"], ["NQ%d" % h], 8)
-        v(ts(T.PQ[:, h:h + 1], T.PI2[:, 1:2], -16.0 * h, None, A.add), ["PI3"], ["PQ%d" % h], 8)
-        v(ts(T.TRI[:, 128 * h:128 * h + 128], T.IK[:], T.PQ[:, h:h + 1], 4096.0, A.is_lt, A.mult), ["IK", "PQ%d" % h], ["TRI%d" % h], 64)
-    gp(iota(T.BLI[:, 24:40], [[0, 2], [1, 8]], 0, 0, False), [], ["BLI2"], 16)
-    v(cp(T.BL[:], T.BLI[:]), ["BLI", "BLI2"], ["BL"], 40)
+        sel(T.BK0[:, s], "BK0%d" % h, T.OFF[:], ["OFF"], [[-32, 4], [0, 32]], A.is_ge, -16 * h, 1)
+        sel(T.BLK[:, s], "BLK%d" % h, T.BK0[:, s], ["BK0%d" % h], [[32, 4], [0, 32]], A.is_ge, 16 * h + 15, -1)
+    sel(T.B31[:], "B31", T.B30[:], ["B300", "B301"], [[0, 2], [-32, 4]], A.is_ge, 0, 1, 8)
+    sel(T.B32[:], "B32", T.B31[:], ["B31"], [[0, 2], [32, 4]], A.is_ge, 31, -1, 8)
+    for i, m in enumerate((15, 31)):
+        v(ts(T.PI[:, i + 1:i + 2], T.PI[:, 0:1], m, None, A.bitwise_and), ["PI"], ["PI%d" % i], 8)
+    v(cp(T.PF[:, 0:2], T.PI[:, 1:3]), ["PI0", "PI1"], ["PF"], 8)
+    lo_, p31 = T.PF[:, 0:1], T.PF[:, 1:2]
+    col = {}
+
+    def times(out, key, src, skey, scale, bias=0.0, n=8, f=AF.Identity):
+        a(act(out, src, f, scale=col.get(scale, scale), bias=bias), [skey] + [scale] * (scale in col), [key], n)
+
+    def number(name, scale, bias, f=AF.Identity):
+        col[name] = T.PF[:, 2 + len(col):3 + len(col)]
+        times(col[name], name, lo_, "PF", scale, bias, f=f)
+    number("w2", 2.0, 1.0)
+    number("low", -1.0, FO - 2.0)
+    number("high", 1.0, FO + 2048.0)
+    number("r1", 2.0, -32.0)
+    number("r2", -1.0, 16.0, AF.Square)
+    number("row0", -1.0, 1.0, AF.Relu)
+    GM = T.GM[:, 0:8]
+    v(cp(T.BL[:], T.BI[:]), ["BI"], ["BL"], 16)
+    v(ts(T.MK[:], T.IK[:, 0:128], lo_, None, A.is_equal), ["IK", "PF"], ["MK"], 64)
+    v(ts(T.TR0[:], T.IK[:], p31, 8192.0, A.subtract, A.mult), ["IK", "PF"], ["TR0"], 128)
+    v(ts(T.TRI[:], T.TR0[:], 1.0, None, A.min), ["TR0"], ["TRI"], 128)
     v(tt(T.DR[:], T.SHF[:], T.REV[:], A.subtract), ["SHF", "REV"], ["DR"], 256)
-    v(ts(T.RST[:], T.KC[:], 0.0, 2.0 ** 25, A.is_equal, A.mult), ["KC"], ["RST"], 256)
-    for c in (0, 1):
-        v(cp(T.TT[:, 768 * c:768 * c + 128], T.IK[:]), ["IK"], ["TTk%d" % c], 64)
-        v(ts(T.TT[:, 768 * c + 384:768 * c + 512], T.IK[:], T.PLO[:], None, A.is_equal), ["IK", "PLO"], ["TTm%d" % c], 64)
+    times(T.NSH[:], "NSH", SH, "SH", -1.0, n=128)
+    times(T.NID[:], "NID", ID, "ID", -1.0, n=128)
+    times(T.WT[:], "WT", GM, "GM", "w2")
+    times(T.GB[:], "GB", GM, "GM", 2048.0)
+    mixed = any(len(set(m)) > 1 for m in cfg["MN"].values())
+    for i, val in enumerate((1.0, -2.0, -1.0, 2.0)[:2 + 2 * mixed]):
+        times(T.PS[:, 24 * i:24 * i + 16], "PS%da" % i, T.GM[:], "GM", val * 65536.0, n=16)
+        times(T.PS[:, 24 * i + 16:24 * i + 24], "PS%db" % i, GM, "GM", -val * 65536.0)
+    for key, m, q, src, scale in (("CTv", 0, QV, "GM", 1.0), ("CTo", 0, Q1, "GM", -1.0), ("CTs", 1, QS, "GB", 1.0), ("CTk", 1, QK, "GB", "r1"),
+                                  ("CTr", 1, Q2, "GB", "r2"), ("CTz", 2, QZ, "GM", "row0")):
+        times(T.CT[:, 64 * m + 8 * q:64 * m + 8 * q + 8], key, T[src][:, 0:8], src, scale)
+        ops[-1]["rd"].append("CT")
+    times(T.CT[:, 128 + 8 * Q1:136 + 8 * Q1], "CTn", T.CT[:, 128 + 8 * QZ:136 + 8 * QZ], "CTz", -1.0)
+    c0, c1, c2 = (T.CT[:, 64 * m:64 * m + 56] for m in range(3))
+    mm("ct", [(T.bM0[0:56, 0:128], c0, ID, True, False, 128), (T.bM0[0:56, 0:128], c1, T.NID[:], False, True, 128),
+              (T.bM0[0:56, 128:256], c0, ID, True, False, 128), (T.bM0[0:56, 128:256], c1, ID, False, True, 128),
+              (T.bM0[0:56, 256:384], c2, ID, True, True, 128),
+              (T.bM0[0:56, 384:512], c0, T.NID[:], True, False, 128), (T.bM0[0:56, 384:512], c1, T.NID[:], False, True, 128)],
+       ["CTv", "CTo", "CTs", "CTk", "CTr", "CTz", "CTn", "ID", "NID"], ["bM0"], "bM0")
+    a(act(T.CQ[0:56, :], T.bM0[0:56, :], AF.Copy), ["bM0"], ["CQ"], 512, ["bM0"])
+    CLO, CHI, CZ, CNH = (T.CQ[0:56, 128 * m:128 * m + 128] for m in range(4))
     for h in range(2):
         s = slice(512 * h, 512 * h + 512)
         a(act(T.F[:, FO + 1024 + 512 * h:FO + 1536 + 512 * h], T.fin[:, s], AF.Identity, bias=-1023.5 / 2048, scale=1.0 / 2048),
@@ -197,326 +241,258 @@ def build(g, T, topo, core, cfg):
     rid, pid = topo.addr(dst, core)
     mask = topo.mask(core, dst)
 
-    def plus(kind, c, out, in_, add, rd, wr, n, banks=()):
-        if cfg[kind][c] == "A":
-            a(act(out, in_, AF.Identity, bias=add) if add else act(out, in_, AF.Copy), rd, wr, n, banks)
-        else:
-            v(ts(out, in_, add, None, A.add) if add else cp(out, in_), rd, wr, n, banks)
-
-    def gather(who, out, win, rd, wr, n):
-        if who == "V":
-            v(cp(out, win), rd, wr, gam * n)
-        else:
-            a(act(out, win, AF.Copy), rd, wr, gam * n)
-
     for t in range(NV):
         now[0] = t
-        dma("S", T.F0[:], T.F[:], FK + ["rec0", "rec1", "WF%d0" % t], ["F0"], 6000)
-        for c in (1, 0):
-            for who, lo, hi in parts(cfg["FG"][c]):
-                w0 = 256 * t + 128 * c
-                gather(who, T.G[:, 2048 * c + 256 * lo:2048 * c + 256 * hi], T.F[:, FO:FO + 2048].indirect(T.WO[:, w0 + 16 * lo:w0 + 16 * hi]),
-                       FK + ["WO%d%d" % (t, c)], ["G%d.%d" % (c, s) for s in range(lo, hi)], 256 * (hi - lo))
+        if cfg["F0"]:
+            dma("S", T.F0[:], T.F[:], FK + ["rec", "rec2", "WF%d0" % t], ["F0"], 6000)
+            call("keep")
         for c in (1, 0):
             C = str(c)
-            w0 = 256 * t + 128 * c
-            x0 = 128 * c
+            w0, x0, g0, k0, p0, q0 = 256 * t + 128 * c, 128 * c, 2048 * c, 512 * c, 48 * c, 64 * c
+            x = slice(x0, x0 + 128)
+            c8 = slice(8 * c, 8 * c + 8)
             WFk, WOk = "WF%d%d" % (t, c), "WO%d%d" % (t, c)
             Wf = T.WF[:, w0:w0 + 128]
-            bK = T["bK" + C]
-            TT0 = 768 * c
-            g0 = 2048 * c
+            BK, BP, BM, BQ = ("b" + b + C for b in "KPMQ")
+            bK, bP, bM, bQ = T[BK], T[BP], T[BM], T[BQ]
             Gk = ["G%d.%d" % (c, s) for s in range(8)]
             Xk = ["X%d.%d" % (c, s) for s in range(8)]
-            b = "bR" + C
-            mm([(T[b][:, 0:128], Wf, T.NSH[:], True, False, 128)], [WFk, "NSH"], [b], b)
+
+            def who(kind, c=c):
+                return cfg[kind][1 - c]
+            if t:
+                plus(who("WO"), T.WO[:, w0:w0 + 128], Wf, 0.0, [WFk], [WOk], 128, half=True)
+                call(who("WO") + "WO" + C)
+            for e, lo, hi in parts(cfg["FG"][c]):
+                gather(e, T.G[:, g0 + 256 * lo:g0 + 256 * hi], T.F[:, FO:FO + 2048].indirect(T.WO[:, w0 + 16 * lo:w0 + 16 * hi]),
+                       FK + [WOk], Gk[lo:hi], 256 * (hi - lo))
+            mm("prev" + C, [(bP[:, 0:128], Wf, T.NSH[:], True, False, 128)], [WFk, "NSH"], [BP + "v"], BP)
             vs = cfg["VS"][c]
             for s in range(vs):
                 m = 128 // vs
-                mm([(T[b][m * s:m * s + m, k:128:16], T.G[:, g0 + 16 * m * s + k:g0 + 16 * m * (s + 1):16], T.ID[:, k:128:16], False,
-                     k == 15, 8) for k in range(16)], Gk[8 // vs * s:8 // vs * (s + 1)] + ["ID"], [b], b, min(m, 64))
-            VT = T.VT[:, x0:x0 + 128]
-            if cfg["VE"][c] == "A":
-                a(act(VT, T[b][:, 0:128], AF.Copy), [b], ["VT" + C], 128, [b])
-            else:
-                v(cp(VT, T[b][:, 0:128]), [b], ["VT" + C], 128, [b])
-            mm([(T.bV[:, 128:256], VT, T.ID[:], True, True, 128)], ["VT" + C, "ID"], ["bVb"], "bV")
-            plus("EO", c, T.EO[:, x0:x0 + 128], T.bV[:, 128:256], 2048.0, ["bVb"], ["EO" + C], 128, ["bV"])
-            for who, lo, hi in parts(cfg["XG"][c]):
-                gather(who, T.X[:, g0 + 256 * lo:g0 + 256 * hi], T.rec2[:, 0:4096].indirect(T.EO[:, x0 + 16 * lo:x0 + 16 * hi]),
-                       ["rec0", "rec1", "EO" + C], Xk[lo:hi], 256 * (hi - lo))
-            v(ts(T.NG[:, x0:x0 + 128], VT, 0.0, 2048.0, A.is_lt, A.mult), ["VT" + C], ["NG" + C], 64)
-            mm([(T.bV[:, 256:384], T.ID[:], VT, True, False, 128), (T.bV[:, 256:384], T.ID[:], T.NG[:, x0:x0 + 128], False, True, 128),
-                (T.bV[:, 384:512], Wf, T.DR[:], True, True, 128)], ["VT" + C, "NG" + C, WFk, "DR", "ID"], ["bVc"], "bV")
-            a(act(T.TT[:, TT0 + 128:TT0 + 384], T.bV[:, 256:512], AF.Copy), ["bVc"], ["TTe" + C, "TTd" + C], 256, ["bV"])
-            BK = "bK" + C
-            mm([(bK[:], T.ONE[0:1, :], T.KC[0:1, :], True, False, 512), (bK[:, 256:384], T.ONE[0:1, :], T.ONE[0:1, :], False, False, 128)],
-               ["ONE", "KC"], [BK], BK)
-            mm([(bK[:, 128:256], Wf, T.SH[:], False, False, 128), (bK[:, 256:384], Wf, T.ID[:], False, False, 128),
-                (bK[:, 384:512], Wf, T.SH[:], False, False, 128)], [WFk, "SH", "ID", BK], [BK + "w"], BK, group=(t, c))
-            mm([(bK[:, 128:256], T.ID[:], VT, False, False, 128), (bK[:, 0:128], T.ID[:], T.TT[:, TT0 + 128:TT0 + 256], False, False, 128)],
-               ["TTe" + C, "VT" + C, "ID", BK], [BK + "e"], BK, group=(t, c))
-        for c in (1, 0):
-            C = str(c)
-            w0 = 256 * t + 128 * c
-            x0 = 128 * c
-            WFk = "WF%d%d" % (t, c)
-            BK = "bK" + C
-            Wf = T.WF[:, w0:w0 + 128]
-            bK = T["bK" + C]
-            TT0 = 768 * c
-            g0 = 2048 * c
-            Xk = ["X%d.%d" % (c, s) for s in range(8)]
-            for h in range(2):
-                mm([(T.bS[:, 64 * h:64 * h + 64], T.ID[:], T.X[:, g0 + 1024 * h + k:g0 + 1024 * h + 1024:16], k == 0, k == 15, 64)
-                    for k in range(16)], Xk[4 * h:4 * h + 4] + ["ID"], ["bS%d" % h], "bS")
-            MB = T.MB[:, x0:x0 + 128]
-            a(act(MB, T.bS[:, 0:128], AF.Identity, bias=192.0 - 15.0 / 32, scale=1.0 / 16), ["bS0", "bS1"], ["MB" + C], 128, ["bS"])
-            mn = cfg["MN"][c]
+                mm("pick" + C, [(bP[m * s:m * s + m, k:128:16], T.G[:, g0 + 16 * m * s + k:g0 + 16 * m * (s + 1):16], ID[:, k:128:16], False,
+                                 k == 15, 8) for k in range(16)], Gk[8 // vs * s:8 // vs * (s + 1)] + ["ID"], [BP + "v"], BP, min(m, 64))
+            VT, NG = T.VT[:, x], T.NG[:, x]
+            plus(who("VT"), VT, bP[:, 0:128], 0.0, [BP + "v"], ["VT" + C], 128, [BP])
+            v(ts(NG, VT, 0.0, 2048.0, A.is_lt, A.mult), ["VT" + C], ["NG" + C], 64)
+            mm("turn" + C, [(bP[:, 128:256], VT, ID, True, cfg["RD"] == 1, 128)] + [(bP[:, 128:256], NG, ID, False, True, 128)] * (1 - cfg["RD"]),
+               ["VT" + C, "ID"] + ["NG" + C] * (1 - cfg["RD"]), [BP + "e"], BP)
+            plus(who("EO"), T.EO[:, x], bP[:, 128:256], 2048.0 * cfg["RD"], [BP + "e"], ["EO" + C], 128, [BP])
+            for e, lo, hi in parts(cfg["XG"][c]):
+                gather(e, T.X[:, g0 + 256 * lo:g0 + 256 * hi], T.R[:, 0:2048 << cfg["RD"]].indirect(T.EO[:, x0 + 16 * lo:x0 + 16 * hi]),
+                       ["rec", "rec2", "EO" + C], Xk[lo:hi], 256 * (hi - lo))
+            TE, TD = T.TT[:, 2 * x0:2 * x0 + 128], T.TT[:, 2 * x0 + 128:2 * x0 + 256]
+            BT = BQ if c else BM
+            tk = [BQ + "s", BQ + "w"] if c else [BM]
+            mm("td" + C, [(T[BT][:, 128:256], Wf, T.DR[:], True, True, 128)], ["DR", WFk], tk, BT)
+            mm("tt" + C, [(T[BT][:, 0:128], ID, VT, True, False, 128), (T[BT][:, 0:128], ID, NG, False, True, 128)], ["VT" + C, "NG" + C, "ID"], tk, BT)
+            plus(who("TT"), T.TT[:, 2 * x0:2 * x0 + 256], T[BT][:, 0:256], 0.0, tk, ["TT" + C, "TD" + C], 256, [BT])
+            ki = cfg["KI"]
+            mm("key" + C, [(bK[:, 384 - ki:384], ONE, KC[:, 384 - ki:384], True, False, ki)], ["ONE", "KC0", "KC"], [BK], BK)
+            mm("kw" + C, [(bK[:, 0:256], Wf, T.IDS[:], False, False, 256)], [WFk, "SH", "ID", BK], [BK + "w"], BK, group=(t, c))
+            mm("ke" + C, [(bK[:, 256:384], ID, TE, False, False, 128)], ["TT" + C, "ID", BK], [BK + "e"], BK, group=(t, c))
+            mn, nh = cfg["MN"][c], cfg["HS"][c]
+            m = 128 // nh
+            QK_ = [BQ + s for s in ("s", "a", "w")]
+            MB = T.MB[:, x]
+            MBk = ["MB%d.%d" % (c, h) for h in range(nh)]
             if "V" in mn:
-                mm([(T.bM[:], T.ONE[0:1, :], T.N192[0:1, :], True, False, 512)], ["ONE", "N192"], ["bM"], "bM")
-                mm([(T.bM[:, s:512:4], T.ID[:], MB, False, s == 3, 128) for s in range(4)], ["MB" + C, "ID"], ["bM"], "bM")
+                mm("n192" + C, [(bM[:], ONE, N192, True, False, 512)], ["ONE", "N192"], [BM], BM)
             nr = 0
+            for h in range(2):
+                mm("sum%d.%d" % (c, h), [(bP[:, 256 + 64 * h:320 + 64 * h], ID, T.X[:, g0 + 1024 * h + k:g0 + 1024 * h + 1024:16], k == 0, k == 15, 64)
+                                         for k in range(16)], Xk[4 * h:4 * h + 4] + ["ID"], [BP + "s%d" % h], BP)
+                if h < 2 - nh:
+                    continue
+                h = h - 2 + nh
+                MBh, Xh = MB[:, m * h:m * h + m], Xk[8 // nh * h:8 // nh * (h + 1)]
+                a(act(MBh, bP[:, 256 + m * h:256 + m * h + m], AF.Identity, bias=192.0 - 15.0 / 32, scale=1.0 / 16),
+                  [BP + "s0", BP + "s1"][h:h + 3 - nh], [MBk[h]], m, [BP])
+                if "V" in mn:
+                    mm("wide%d.%d" % (c, h), [(bM[:, 4 * m * h + s:4 * m * (h + 1):4], ID, MBh, False, s == 3 and h == nh - 1, m) for s in range(4)],
+                       [MBk[h], "ID", BM], [BM + "h%d" % h], BM)
+                for j in range(4):
+                    Xj = T.X[:, g0 + 16 * m * h + j:g0 + 16 * m * (h + 1):4]
+                    MXj = T.MX[:, g0 + 512 * j + 4 * m * h:g0 + 512 * j + 4 * m * (h + 1)]
+                    MXk = "MX%d.%d.%d" % (c, j, h)
+                    if mn[j] == "V":
+                        v(tt(MXj, Xj, bM[:, 4 * m * h:4 * m * (h + 1)], A.min), Xh + [BM, BM + "h%d" % h], [MXk], 4 * m, [BM])
+                    else:
+                        b = [BQ, BP if h == nh - 1 else BQ][nr % 2] if "V" in mn else ([BQ, BM, BP] if h == nh - 1 else [BQ, BM, BQ])[nr % cfg["NB"]]
+                        bk = QK_ if b == BQ else [BP + s for s in ("v", "e", "s0", "s1", "u", "l", "o")] if b == BP else [b]
+                        nr += 1
+                        mm("x%d.%d.%d" % (c, j, h), [(T[b][:, 0:4 * m], ID, Xj, True, False, 4 * m)], Xh + ["ID"], bk, b)
+                        mm("sub%d.%d.%d" % (c, j, h), [(T[b][:, s:4 * m:4], T.NID[:], MBh, False, s == 3, m) for s in range(4)],
+                           [MBk[h], "NID"], bk, b)
+                        a(act(MXj, T[b][:, 0:4 * m], AF.Relu if "V" in mn else AF.Abs, bias=192.0), bk, [MXk], 4 * m, [b])
+            mm("u" + C, [(bP[:, 392:400], MB, T.WT[:], True, True, 8)], MBk + ["WT"], [BP + "u"], BP)
+            a(act(T.U2[:, c8], bP[:, 392:400], AF.Square, bias=592.0 - 192.0 * 256), [BP + "u"], ["U2" + C], 8, [BP])
+            a(act(T.KS[:, k0 + 399:k0 + 512:16], T.U2[:, c8], AF.Identity, bias=-712.4375, scale=1.0 / 32), ["U2" + C], ["KZ" + C], 8)
             for j in range(4):
-                Xj = T.X[:, g0 + j:g0 + 2048:4]
-                MXj = T.MX[:, g0 + 512 * j:g0 + 512 * j + 512]
-                MXk = "MX%d.%d" % (c, j)
-                if mn[j] == "V":
-                    v(tt(MXj, Xj, T.bM[:], A.min), Xk + ["bM"], [MXk], 512, ["bM"])
-                else:
-                    b = (["bR0", "bR1"] * 2 if c else ["bR0", "bR1", "bV", "bM"])[nr]
-                    bk = ["bVb", "bVc"] if b == "bV" else [b]
-                    nr += 1
-                    mm([(T[b][:], T.ID[:], Xj, True, False, 512)], Xk + ["ID"], bk, b)
-                    mm([(T[b][:, s:512:4], T.NID[:], MB, False, s == 3, 128) for s in range(4)], ["MB" + C, "NID"], bk, b)
-                    a(act(MXj, T[b][:], AF.Relu if "V" in mn else AF.Abs, bias=192.0), bk, [MXk], 512, [b])
-            for j in range(4 if "V" in mn else 0):
-                mm([(bK[:, k:512:16], T.X[:, g0 + k:g0 + 2048:16], T.PS[:, 0:32] if mn[j] == "V" else T.PS[:, 64:96], False, False, 32)
-                    for k in range(j, 16, 4)], Xk + ["PS", BK], [BK + "x%d" % j], BK, group=(t, c))
-            mm([(T.bS[:, 128:136], MB, T.WT[:], True, True, 8)], ["MB" + C, "WT"], ["bSu"], "bS")
-            c8 = slice(8 * c, 8 * c + 8)
-            a(act(T.U2[:, c8], T.bS[:, 128:136], AF.Square, bias=592.0 - 192.0 * 256), ["bSu"], ["U2" + C], 8, ["bS"])
-            plus("Z1", c, T.Z1[:, c8], T.U2[:, c8], 42752.0, ["U2" + C], ["Z1" + C], 8)
-            v(ts(T.ZI[:, c8], T.Z1[:, c8], 5, 2047, A.arith_shift_right, A.bitwise_and), ["Z1" + C], ["ZI" + C], 8)
-            plus("ZT", c, T.ZT[:, x0:x0 + 128:16], T.ZI[:, c8], 0.0, ["ZI" + C], ["ZT" + C], 8)
-            for j in range(4):
-                mm([(bK[:, j + 4 * kk:512:16], T.MX[:, g0 + 512 * j + kk:g0 + 512 * j + 512:4],
-                     T.PS[:, 32:64] if mn[j] == "V" else T.PS[:, 96:128] if "V" in mn else T.PS[:, 0:32], False, False, 32) for kk in range(4)],
-                   ["MX%d.%d" % (c, j), "PS", BK, BK + "x%d" % j], [BK + "m%d" % j], BK, group=(t, c))
-            KS = T.KS[:, 512 * c:512 * c + 512]
-            v(lambda KS=KS, bK=bK: V.tensor_tensor_scan(KS, T.RST[:], bK[:], 0.0, A.add, A.min),
-              ["RST", BK, BK + "w", BK + "e"] + [BK + "m%d" % j for j in range(4)], ["KS" + C], 512, [BK])
-            k0, p0, s0 = 512 * c, 40 * c, 32 * c
-            v(ts(T.PL[:, p0 + 8:p0 + 40], T.KS[:, k0 + 15:k0 + 512:16], 4095, None, A.bitwise_and), ["KS" + C], ["PL" + C], 32)
-            v(ts(T.PL[:, p0:p0 + 8], T.KS[:, k0 + 143:k0 + 256:16], 12, 15, A.arith_shift_right, A.bitwise_and), ["KS" + C], ["PK" + C], 8)
-            n_, f_, col_, pv_ = (T.PL[:, p0 + 8 * i:p0 + 8 * i + 8] for i in (1, 2, 3, 4))
-            if cfg["TO"][c]:
-                v(tt(T.TT[:, TT0 + 640:TT0 + 768], n_.indirect(T.BL[:, 0:8]), T.TT[:, TT0 + 128:TT0 + 256], A.is_equal),
-                  ["PL" + C, "BL", "TTe" + C], ["TTq" + C], gam * 128)
-                v(tt(T.TT[:, TT0 + 512:TT0 + 640], T.PL[:, p0:p0 + 8].indirect(T.BL[:, 0:8]), T.TT[:, TT0:TT0 + 128], A.is_equal),
-                  ["PK" + C, "BL", "TTk" + C], ["TTo" + C], gam * 128)
+                i = 0 if mn[j] == "V" else 2
+                if "V" in mn:
+                    mm("kx%d.%d" % (c, j), [(bK[:, k:384:16], T.X[:, g0 + k:g0 + 2048:16], T.PS[:, 24 * i:24 * i + 24], False, False, 24)
+                                            for k in range(j, 16, 4)], Xk + ["PS%da" % i, "PS%db" % i, BK, BK + "w"], [BK + "x%d" % j], BK,
+                       group=(t, c))
+                i = i + 1 if "V" in mn else 0
+                mm("km%d.%d" % (c, j), [(bK[:, j + 4 * kk:384:16], T.MX[:, g0 + 512 * j + kk:g0 + 512 * j + 512:4], T.PS[:, 24 * i:24 * i + 24],
+                                         False, False, 24) for kk in range(4)],
+                   ["MX%d.%d.%d" % (c, j, h) for h in range(nh)] + ["PS%da" % i, "PS%db" % i, BK, BK + "w", BK + "x%d" % j], [BK + "m%d" % j], BK,
+                   group=(t, c))
+            KK = [BK, BK + "w", BK + "e"] + [BK + s + str(j) for s in "xm" for j in range(4)]
+            v(scan(T.KS[:, k0:k0 + 256], T.RST[:], bK[:, 128:384], A.add, A.max), ["RST"] + KK, ["KS" + C], 256, [BK])
+            v(scan(T.KP[:, x], T.RST[:, 0:128], bK[:, 0:128], A.add, A.max), ["RST"] + KK, ["KP" + C], 128, [BK])
+            sums = T.KS[:, k0 + 271:k0 + 384:16]
+            col_, n_, z_ = (T.PL[:, p0 + 8 * i:p0 + 8 * i + 8] for i in (0, 1, 3))
+            v(ts(T.PL[:, p0:p0 + 16], T.KS[:, k0 + 15:k0 + 256:16], 2047, None, A.bitwise_and), ["KS" + C], ["PL" + C], 16)
+            v(tt(sums, T.KP[:, x0 + 15:x0 + 128:16], T.KS[:, k0 + 143:k0 + 256:16], A.add), ["KS" + C, "KP" + C], ["T1" + C], 16)
+            v(ts(T.PL[:, p0 + 32:p0 + 40], T.KS[:, k0 + 15:k0 + 128:16], 11, 15, A.arith_shift_right, A.bitwise_and), ["KS" + C], ["PK" + C], 8)
+            v(ts(T.PL[:, p0 + 16:p0 + 32], T.KS[:, k0 + 271:k0 + 512:16], 2047, None, A.bitwise_and), ["T1" + C, "KZ" + C], ["PV" + C], 16)
+            v(tt(T.PL[:, p0 + 40:p0 + 48], col_, sums, A.min), ["PL" + C, "T1" + C], ["PC" + C], 16)
+            QW = T.QW[:, q0:q0 + 56]
+            rd = ["PV" + C, "PK" + C, "PC" + C]
+            if who("QW") == "V":
+                v(ts(QW[:, 0:32], T.PL[:, p0 + 16:p0 + 48], 1.0, 0.0, A.add, A.max), rd, ["QW" + C], 32)
             else:
-                v(tt(T.TT[:, TT0 + 512:TT0 + 768], T.PL[:, p0:p0 + 16].indirect(T.BL[:, 0:16]), T.TT[:, TT0:TT0 + 256], A.is_equal),
-                  ["PL" + C, "PK" + C, "BL", "TTk" + C, "TTe" + C], ["TTo" + C, "TTq" + C], gam * 256)
-            v(tt(T.T1[:, c8], n_, pv_, A.add), ["PL" + C], ["T1" + C], 16)
-            v(lambda c=c, TT0=TT0: V.tensor_tensor_scan(T.SS[:, 128 * c:128 * c + 128], T.KEEP[:], T.TT[:, TT0 + 640:TT0 + 768], 0.0,
-                                                        A.mult, A.add), ["KEEP", "TTq" + C], ["SS" + C], 128)
-            v(ts(T.T2[:, c8], T.T1[:, c8], 2047, None, A.bitwise_and), ["T1" + C], ["T2" + C], 8)
-            go, t4, dl, cw = (T.SM[:, s0 + 8 * i:s0 + 8 * i + 8] for i in range(4))
-            v(tt(dl, T.T2[:, c8], f_, A.subtract), ["T2" + C, "PL" + C], ["dl" + C], 16)
-            v(ts(go, T.SS[:, x0 + 15:x0 + 128:16], T.PAR[:], 6.0, A.subtract, A.is_ge), ["SS" + C, "PAR"], ["go" + C], 8)
-            v(ts(T.T3[:, c8], dl, 0.0, None, A.not_equal), ["dl" + C], ["T3" + C], 8)
-            v(tt(T.TT[:, TT0 + 256:TT0 + 384:16], n_, T.ZI[:, c8], A.subtract), ["PL" + C, "ZI" + C], ["TTd" + C], 16)
-            v(tt(t4, T.T3[:, c8], col_, A.mult), ["T3" + C, "PL" + C], ["T4" + C], 16)
-            v(tt(cw, t4, go, A.mult), ["T4" + C, "go" + C], ["cw" + C], 16)
-            o0 = 384 * c
-            mk = [["go" + C, "TTd" + C], ["PL" + C, "TTm" + C], ["dl" + C, "TTo" + C]]
-            for i, col in enumerate((go, col_, dl)):
-                o1, i1 = o0 + 128 * i, TT0 + 256 + 128 * i
-                if cfg["MO"][c][i] == "V":
-                    v(tt(T.MO[:, o1:o1 + 128], col.indirect(T.BL[:, 0:8]), T.TT[:, i1:i1 + 128], A.mult), mk[i] + ["BL"], ["MO%d.%d" % (c, i)],
-                      gam * 128)
-                else:
-                    def scaled(o1=o1, i1=i1, s1=s0 + 8 * i):
-                        r = None
-                        for q in range(8):
-                            r = S.activation(T.MO[:, o1 + 16 * q:o1 + 16 * q + 16], T.TT[:, i1 + 16 * q:i1 + 16 * q + 16], AF.Copy,
-                                             scale=T.SM[:, s1 + q:s1 + q + 1])
-                        return r
-                    op("A", scaled, mk[i], ["MO%d.%d" % (c, i)], 8 * 80)
-            M0, M1, M2 = ("MO%d.%d" % (c, i) for i in range(3))
-            Dm = T.MO[:, o0 + 128:o0 + 256]
-            BK = "bK" + C
-            mm([(bK[:, 0:256], T.ID[:], T.TRI[:], True, False, 256)], ["ID", "TRI0", "TRI1"], [BK], BK)
-            mm([(bK[:, 128 * h:128 * h + 128], T.BLK[:, 128 * h:128 * h + 128], Dm, False, h == 1, 128) for h in range(2)],
-               [M1, "BLK0", "BLK1"], [BK], BK)
-            mm([(bK[:, 376:384], T.ONE[0:1, :], T.C31[0:1, :], True, False, 8), (bK[:, 376:384], Dm, T.PS[:, 136:144], False, True, 8)],
-               [M1, "PS", "ONE", "C31"], [BK], BK)
-            if cfg["EQ"][c] == "V":
-                a(act(T.BM[:, 2 * x0:2 * x0 + 256], bK[:, 0:256], AF.Copy), [BK], ["BM" + C], 256, [BK])
-            else:
-                gather("A", T.BM[:, 2 * x0:2 * x0 + 256], cw.indirect(T.BL[:, 24:40]), ["cw" + C, "BL"], ["BM" + C], 256)
-            plus("LO", c, T.LO[:, c8], bK[:, 376:384], 0.0, [BK], ["LO" + C], 8, [BK])
-            gather("A", T.OLD[:, x0:x0 + 128], (T.F if c else T.F0)[:].indirect(T.LO[:, c8]), (FK if c else ["F0"]) + ["LO" + C], ["OLD" + C], 128)
-            mm([(T.bT[:, 0:128], T.REV[:], Wf, True, False, 128), (T.bT[:, 0:128], T.ZT[:, x0:x0 + 128], T.ID[:], False, False, 128),
-                (T.bT[:, 0:128], T.MO[:, o0:o0 + 128], T.ID[:], False, True, 128)], ["REV", WFk, "ZT" + C, M0, "ID"], ["bTa"], "bT")
-            mm([(T.bT[:, 128:256], T.MO[:, o0 + 256:o0 + 384], T.ID[:], True, False, 128),
-                (T.bT[:, 128:256], T.ID[:], T.OLD[:, x0:x0 + 128], False, True, 128)], [M2, "ID", "OLD" + C], ["bTb"], "bT")
-            if cfg["EQ"][c] == "V":
-                v(tt(T.EQ[:, 2 * x0:2 * x0 + 256], cw.indirect(T.BL[:, 24:40]), T.BM[:, 2 * x0:2 * x0 + 256], A.is_equal),
-                  ["cw" + C, "BL", "BM" + C], ["EQ" + C], gam * 256)
-            else:
-                v(tt(T.EQ[:, 2 * x0:2 * x0 + 256], bK[:, 0:256], T.BM[:, 2 * x0:2 * x0 + 256], A.is_equal), ["BM" + C, BK], ["EQ" + C], 256, [BK])
-            mm([(bK[:, 384:392], T.ONE[0:1, :], T.C31[0:1, :], True, False, 8), (bK[:, 384:392], Dm, T.PS[:, 136:144], False, False, 8)]
-               + [(bK[:, 384 + h:392:2], T.EQ[:, 2 * x0 + 128 * h:2 * x0 + 128 * h + 128], T.B32[:, 4 * h:4 * h + 4], False, h == 1, 4)
-                  for h in range(2)], ["EQ" + C, "B32", M1], [BK], BK)
+                a(act(QW[:, 0:32], T.PL[:, p0 + 16:p0 + 48], AF.Relu, bias=1.0), rd, ["QW" + C], 32)
+            a(act(QW[:, 32:40], T.PL[:, p0 + 32:p0 + 40], AF.Square, bias=1.0), ["PK" + C], ["QS" + C], 8)
+            mm("q" + C, [(bQ[0:56, 0:128], QW, ID, True, True, 128)], ["QW" + C, "QS" + C, "ID"], [BQ + "s"], BQ)
+            QT = T.QT[0:56, x]
+            plus(who("QT"), QT, bQ[0:56, 0:128], 0.0, [BQ + "s"], ["QT" + C], 128, [BQ])
+            DM, SS, OLD, PR, EQ = T.DM[:, x], T.SS[:, x], T.OLD[:, x], T.PR[:, x], T.EQ[:, 2 * x0:2 * x0 + 256]
+            v(tt(DM, col_.indirect(T.BL[:, 0:8]), T.MK[:], A.mult), ["PL" + C, "BL", "MK"], ["DM" + C], gam * 128)
+            mm("lo" + C, [(bP[:, 400:408], DM, GM, True, True, 8)], ["DM" + C, "GM"], [BP + "o"], BP)
+            plus(who("LO"), T.LO[:, c8], bP[:, 400:408], FO + 0.0, [BP + "o"], ["LO" + C], 8, [BP])
+            kept = cfg["F0"] and c == 0
+            gather(who("OLD"), OLD, (T.F0 if kept else T.F)[:].indirect(T.LO[:, c8]), (["F0"] if kept else FK) + ["LO" + C], ["OLD" + C], 128)
+            out, okey = (T.SF[:, w0:w0 + 128], "SF%d%d" % (t, c)) if t < NV - 1 else (T.YW[:, x], "YW" + C)
+            go, cw = T.SM[:, 32 * c:32 * c + 8], T.SM[:, 32 * c + 8:32 * c + 16]
+            BS = T.BS[:, 2 * x0:2 * x0 + 256]
+            v(tt(T.EV[:, x], n_.indirect(T.BL[:, 0:8]), TE, A.is_equal), ["PL" + C, "BL", "TT" + C], ["EV" + C], gam * 128)
+            v(scan(SS, T.KEEP[:], T.EV[:, x], A.mult, A.add), ["KEEP", "EV" + C], ["SS" + C], 64)
+            v(ts(go, SS[:, 15:128:16], T.NP[:], 6.0, A.add, A.is_ge), ["SS" + C, "NP"], ["GO" + C], 8)
+            v(tt(cw, QW[:, 8 * QC:8 * QC + 8], go, A.mult), ["QW" + C, "GO" + C], ["CW" + C], 16)
+            v(tt(TD[:, 0:128:16], n_, z_, A.subtract), ["PL" + C, "PV" + C], ["TD" + C], 16)
             if t < NV - 1:
-                w1 = w0 + 256
-                plus("SO", c, T.SO[:, w0:w0 + 128], T.bT[:, 0:128], 0.0, ["bTa"], ["SO%d%d" % (t, c)], 128, ["bT"])
-                a(act(T.SF[:, w0:w0 + 128], T.bT[:, 0:128], AF.Copy), ["bTa"], ["SF%d%d" % (t, c)], 128, ["bT"])
-                for k in "OF":
-                    arr = "arr%s%d%d" % (k, t + 1, c)
-                    op("G", lambda k=k, w0=w0, w1=w1, arr=arr: g.remote_dma(T["W" + k][:, w1:w1 + 128], T["S" + k][:, w0:w0 + 128], T.sem[arr],
-                                                                            T.sem.sent, pid, rid, mask),
-                       ["S%s%d%d" % (k, t, c)], ["W%s%d%d" % (k, t + 1, c)], 300, (), 2300, arr, -1)
-            else:
-                a(act(T.YW[:, x0:x0 + 128], T.bT[:, 0:128], AF.Copy), ["bTa"], ["YW" + C], 128, ["bT"])
-                dma("S", T.yw[:, x0:x0 + 128], T.YW[:, x0:x0 + 128], ["YW" + C], ["yw" + C], 2000)
-            a(act(T.DL[:, x0:x0 + 128], T.bT[:, 128:256], AF.Copy), ["bTb"], ["DL" + C], 128, ["bT"])
-            v(ts(T.LG[:, c8], bK[:, 384:392], T.NQ[:, 0:1], T.NQ[:, 1:2], A.max, A.min), [BK, "NQ0", "NQ1"], ["LG" + C], 8, [BK])
-            LGk = ["LG" + C]
+                a(act(T.SM[:, 32 * c + 16:32 * c + 24], go, AF.Copy, accum_out=T.AC[:, c:c + 1]), ["GO" + C], ["AC" + C], 32)
+            if who("DL") == "V":
+                mm("bound" + C, [(bM[:, 256:384], CLO, QT, True, True, 128), (bM[:, 384:512], CHI, QT, True, True, 128)], ["QT" + C, "CQ"],
+                   [BM, BM + "h0", BM + "h1"], BM)
+            v(tt(PR, go.indirect(T.BL[:, 0:8]), TD, A.mult), ["GO" + C, "BL", "TD" + C], ["PR" + C], gam * 128)
+            mm("win" + C, [(bQ[:, 128:256], T.REV[:], Wf, True, False, 128), (bQ[:, 128:256], CZ, QT, False, False, 128)],
+               ["REV", WFk, "QT" + C, "CQ"], [BQ + "w"], BQ)
+            mm("new" + C, [(bQ[:, 128:256], PR, ID, False, True, 128)], ["PR" + C, "ID"], [BQ + "w"], BQ)
+            plus(who("SF"), out, bQ[:, 128:256], 0.0, [BQ + "w"], [okey], 128, [BQ])
+            call(who("SF") + "SF" + C)
             if t < NV - 1:
-                op("P", lambda c=c, go=go: PE.matmul(T.bS[:, 144 + 8 * c:152 + 8 * c], T.ONEF[:], go, True, True),
-                   ["ONEF", "go" + C], ["bSa" + C], 256 * pe, ["bS"])
-            for j in range(3, -1, -1):
-                s = slice(x0 + 32 * j, x0 + 32 * j + 32)
-                v(cp(T.F[:].indirect(T.LG[:, 8 * c + 2 * j:8 * c + 2 * j + 2]), T.DL[:, s]), LGk + ["DL" + C], FK, sig * 32)
+                arr = "arr%d%d" % (t + 1, c)
+                op("G", lambda w0=w0, arr=arr: g.remote_dma(T.WF[:, w0 + 256:w0 + 384], T.SF[:, w0:w0 + 128], T.sem[arr], T.sem.sent,
+                                                            pid, rid, mask),
+                   [okey], ["WF%d%d" % (t + 1, c)], 300, (), cfg["far"] + cfg["far0"] * (t == 0 and c == 1), arr, -1)
+            else:
+                dma("S", T.yw[:, x], out, [okey], ["yw" + C], 2000)
+            call("send" + C)
+            mm("tri" + C, [(bK[:, 0:256], ID, T.TRI[:], True, False, 256)], ["ID", "TRI"], KK, BK)
+            mm("blk" + C, [(bK[:, 128 * h:128 * h + 128], T.BLK[:, 128 * h:128 * h + 128], DM, False, h == 1, 128) for h in range(2)],
+               ["DM" + C, "BLK0", "BLK1"], [BK], BK)
+            if who("EQ") == "V":
+                plus(who("BS"), BS, bK[:, 0:256], 0.0, [BK], ["BS" + C], 256, [BK])
+                v(tt(EQ, cw.indirect(T.BL[:]), BS, A.is_equal), ["CW" + C, "BL", "BS" + C], ["EQ" + C], gam * 256)
+            else:
+                gather("A", BS, cw.indirect(T.BL[:]), ["CW" + C, "BL"], ["BW" + C], 256)
+                v(tt(EQ, bK[:, 0:256], BS, A.is_equal), ["BW" + C, BK], ["EQ" + C], 256, [BK])
+            if who("DL") == "V":
+                v(tt(T.CL[:, x], bM[:, 256:384], OLD, A.max), [BM, "OLD" + C], ["CL" + C], 128, [BM])
+                v(tt(T.DL[:, x], bM[:, 384:512], T.CL[:, x], A.min), [BM, "CL" + C], ["DL" + C], 128, [BM])
+            else:
+                RL = T.RL[:, 2 * x0:2 * x0 + 256]
+                mm("over" + C, [(bM[:, 0:128], CLO, QT, True, False, 128), (bM[:, 0:128], T.NID[:], OLD, False, True, 128),
+                                (bM[:, 128:256], CNH, QT, True, False, 128), (bM[:, 128:256], ID, OLD, False, True, 128)],
+                   ["QT" + C, "CQ", "OLD" + C, "ID", "NID"], [BM, BM + "h0", BM + "h1"], BM)
+                a(act(RL, bM[:, 0:256], AF.Relu), [BM], ["RL" + C], 256, [BM])
+                mm("mend" + C, [(bM[:, 256:384], ID, OLD, True, False, 128), (bM[:, 256:384], ID, RL[:, 0:128], False, False, 128),
+                                (bM[:, 256:384], T.NID[:], RL[:, 128:256], False, True, 128)], ["RL" + C, "OLD" + C, "ID", "NID"], [BM], BM)
+                a(act(T.DL[:, x], bM[:, 256:384], AF.Copy), [BM], ["DL" + C], 128, [BM])
+            mm("list" + C, [(bP[:, 384:392], ONE, C32, True, False, 8), (bP[:, 384:392], DM, GM, False, False, 8)], ["DM" + C, "GM", "ONE", "C32"],
+               [BP + "l"], BP)
+            mm("void" + C, [(bP[:, 384 + h:392:2], EQ[:, 128 * h:128 * h + 128], T.B32[:, 4 * h:4 * h + 4], False, h == 1, 4) for h in range(2)],
+               ["EQ" + C, "B32"], [BP + "l"], BP)
+            v(ts(T.LG[:, c8], bP[:, 384:392], col["low"], col["high"], A.max, A.min), [BP + "l", "low", "high"], ["LG" + C], 8, [BP])
+        for j in range(7, -1, -1):
+            v(cp(T.F[:].indirect(T.LG[:, 2 * j:2 * j + 2]), T.DL[:, 32 * j:32 * j + 32]), ["LG%d" % (j // 4), "DL%d" % (j // 4)], FK, sig * 32)
+            call("Vput%d" % j)
         if t < NV - 1:
-            a(act(T.AJ[:], T.bS[:, 144:160], AF.Copy, accum_out=T.AS[:]), ["bSa0", "bSa1"], ["AS"], 40, ["bS"])
-            plus("Z1", 0, T.AI[:], T.AS[:], 0.0, ["AS"], ["AI"], 8)
-            v(ts(T.AP1[:], T.AI[:], 1, None, A.bitwise_and), ["AI"], ["AP1"], 8)
-            plus("ZT", 0, T.PAR[:], T.AP1[:], 0.0, ["AP1"], ["PAR"], 8)
+            back = T.bQ0[:, 400:401]
+            mm("back", [(back, T.CF[:], T.AC[:, c:c + 1], c == 0, c == 1, 256) for c in range(2)], ["CF", "AC0", "AC1"], ["bQ0a"], "bQ0")
+            v(ts(T.AR[:], back, -0.5, MAGIC, A.add, A.add), ["bQ0a"], ["AR"], 8, ["bQ0"])
+            v(ts(T.NP[:], T.AR[:], MAGIC, back, A.subtract, A.subtract), ["bQ0a", "AR"], ["NP"], 8, ["bQ0"])
     now[0] = NV
-    for h, b in enumerate(("bR0", "bR1", "bM", "bK1")):
+    for h, b in enumerate(("bK1", "bM1", "bQ1", "bM0")):
         s = slice(256 * h, 256 * h + 256)
-        a(act(T[b][:, 0:256], T.F[:, FO + 1024 + 256 * h:FO + 1280 + 256 * h], AF.Identity, scale=2048.0), FK, [b], 256, [b])
-        v(tt(T.Y[:, s], T.F[:, FO + 256 * h:FO + 256 * h + 256], T[b][:, 0:256], A.add), FK + [b], ["Y%d" % (h // 2), "Yq%d" % h], 256, [b])
-        dma("S", T.yf[:, s], T.Y[:, s], ["Yq%d" % h], ["yf%d" % h], 2100)
+        keys = [b] + ([b + "s", b + "w"] if b == "bQ1" else [])
+        a(act(T[b][:, 0:256], T.F[:, FO + 1024 + 256 * h:FO + 1280 + 256 * h], AF.Identity, scale=2048.0), FK, keys, 256, [b])
+        v(tt(T.Y[:, s], T.F[:, FO + 256 * h:FO + 256 * h + 256], T[b][:, 0:256], A.add), FK + [b], ["Y%d" % h], 256, [b])
+        dma("S", T.yf[:, s], T.Y[:, s], ["Y%d" % h], ["yf%d" % h], 2100)
     return ops
 
 
-def arrange(ops, cfg):
-    n = len(ops)
-    lastw, readers = {}, {}
+def depend(ops):
+    lastw, readers, seen = {}, {}, {}
+    for o in ops:
+        k = o["name"] or (o["q"] if o["t"] >= 0 else o["q"].lower()) + o["wr"][0]
+        seen[k, o["t"]] = seen.get((k, o["t"]), 0) + 1
+        o["name"] = k + ("" if seen[k, o["t"]] == 1 else "#%d" % seen[k, o["t"]])
     for i, o in enumerate(ops):
-        raw, other = set(), set()
+        dep = set()
         for k in o["rd"]:
             if k in lastw:
-                raw.add(lastw[k])
+                dep.add(lastw[k])
         for k in o["wr"]:
             if k in lastw:
-                other.add(lastw[k])
-            other.update(readers.get(k, ()))
-        other.discard(i)
-        o["raw"], o["dep"] = raw, raw | other
+                dep.add(lastw[k])
+            dep.update(readers.get(k, ()))
+        dep.discard(i)
+        o["dep"] = dep
         for k in o["rd"]:
             readers.setdefault(k, set()).add(i)
         for k in o["wr"]:
             lastw[k] = i
             readers[k] = set()
-    seen = {}
-    for o in ops:
-        k = ".".join(w[:2] + w[3] if w[:2] in ("SO", "SF", "WO", "WF") else w for w in (o["wr"][0], (o["rd"] + [""])[0]))
-        seen[k, o["t"]] = seen.get((k, o["t"]), 0) + 1
-        o["name"] = k + ("" if seen[k, o["t"]] == 1 else "#%d" % seen[k, o["t"]])
-    if cfg.get("places"):
-        cfg = dict(cfg, pos=dict(zip(sorted({o["name"] for o in ops}), [20 * int(x) for x in cfg["places"].split()])))
-    if cfg["pos"]:
-        return replay(ops, cfg)
-    wake = cfg["wake"]
-    succ = [[] for _ in range(n)]
-    for i, o in enumerate(ops):
-        for d in o["dep"]:
-            succ[d].append(i)
-    way = [0.0] * n
-    for i in range(n - 1, -1, -1):
-        way[i] = ops[i]["cost"] + ops[i]["lat"] + max([way[s] + wake for s in succ[i]] + [0.0])
-    seen = {}
-    for i, o in enumerate(ops):
-        way[i] = cfg["look"] * way[i]
-    left = [len(o["dep"]) for o in ops]
-    ready = [i for i in range(n) if left[i] == 0]
-    free, end, bank = {}, [0.0] * n, {}
-    order = []
-
-    def waits(i, d):
-        o, p = ops[i], ops[d]
-        return p["q"] != o["q"] or p["sem"] is not None or (o["q"] != "P" and (d in o["raw"] or cfg["same"]))
-
-    while ready:
-        best = None
-        for i in ready:
-            o = ops[i]
-            st = free.get(o["q"], 0.0)
-            for d in o["dep"]:
-                if waits(i, d):
-                    st = max(st, end[d] + wake)
-            for b in o["banks"]:
-                for (q, d) in bank.get(b, {}).items():
-                    if q != o["q"]:
-                        st = max(st, end[d] + wake)
-            key = (st - way[i], i)
-            if best is None or key < best[0]:
-                best = (key, i, st)
-        _, i, st = best
-        o = ops[i]
-        for b in o["banks"]:
-            for (q, d) in bank.setdefault(b, {}).items():
-                if q != o["q"]:
-                    o["dep"].add(d)
-            bank[b][o["q"]] = i
-        o["wait"] = [d for d in o["dep"] if waits(i, d)]
-        o["start"] = st
-        free[o["q"]] = st + o["cost"]
-        end[i] = st + o["cost"] + o["lat"]
-        order.append(i)
-        ready.remove(i)
-        for s in succ[i]:
-            left[s] -= 1
-            if left[s] == 0:
-                ready.append(s)
-    return order, max(end)
 
 
-def replay(ops, cfg):
-    n = len(ops)
-    key = [-1e6 if o["t"] < 0 and o["sem"] else max(o["t"], 0) * 20000 + cfg["pos"][o["name"]] for o in ops]
-    succ = [[] for _ in range(n)]
+def places(ops, visit, first):
+    at = {w.rstrip("+-"): i + len(visit) * (w.count("+") - w.count("-")) for i, w in enumerate(visit)}
+    ahead, here = {}, len(visit)
+    for w in reversed(first):
+        here = at[w[1:]] if w[0] == "@" else here - 0.001
+        ahead[w] = here
+    return [ahead[o["name"]] if o["t"] < 0 else o["t"] * len(visit) + at[o["name"]] if o["t"] < NV else (NV + 1) * len(visit) + i
+            for i, o in enumerate(ops)]
+
+
+def arrange(ops, visit, first):
+    key = places(ops, visit, first)
+    succ = [[] for _ in ops]
     for i, o in enumerate(ops):
         for d in o["dep"]:
             succ[d].append(i)
     left = [len(o["dep"]) for o in ops]
-    ready = [i for i in range(n) if left[i] == 0]
-    free, end, bank, order = {}, [0.0] * n, {}, []
+    ready = [i for i in range(len(ops)) if left[i] == 0]
+    bank, order = {}, []
     while ready:
         i = min(ready, key=lambda j: (key[j], j))
         ready.remove(i)
         o = ops[i]
         for b in o["banks"]:
-            for (q, d) in bank.setdefault(b, {}).items():
-                if q != o["q"]:
-                    o["dep"].add(d)
+            o["dep"].update(d for q, d in bank.setdefault(b, {}).items() if q != o["q"])
             bank[b][o["q"]] = i
-        o["wait"] = [d for d in o["dep"] if ops[d]["q"] != o["q"] or ops[d]["sem"] is not None or o["q"] != "P"]
-        o["start"] = max([free.get(o["q"], 0.0)] + [end[d] + cfg["wake"] for d in o["wait"]])
-        free[o["q"]] = o["start"] + o["cost"]
-        end[i] = free[o["q"]] + o["lat"]
+        o["wait"] = [d for d in o["dep"] if not o["q"] == ops[d]["q"] == "P"]
         order.append(i)
         for s in succ[i]:
             left[s] -= 1
             if left[s] == 0:
                 ready.append(s)
-    return order, max(end)
+    return order
 
 
 def rank_program(g, core, T, topo):
@@ -524,7 +500,8 @@ def rank_program(g, core, T, topo):
     if rank is None:
         return
     ops = build(g, T, topo, core, CFG)
-    order, _ = arrange(ops, dict(CFG, places=PLACES))
+    depend(ops)
+    order = arrange(ops, CFG["visit"].split(), CFG["first"].split())
     queue = {"V": g.vector, "A": g.scalar, "P": g.tensor, "G": g, "S": g.sync}
     pos = {i: p for p, i in enumerate(order)}
     known = {q: {} for q in queue}

from concourse.mybir import AluOpType as A, ActivationFunctionType as AF

NV = 4
FO = 32
MAGIC = 1.5 * 2.0 ** 24
QV, QZ, QK, QC, QS, Q1, Q2 = range(7)

SCRATCH = {
    "fin": ("sbuf", [128, 1024], "int32"), "wi": ("sbuf", [128, 256], "int32"),
    "Y": ("sbuf", [128, 1024], "float32"), "F": ("sbuf", [128, FO + 2064], "int32"), "R": ("sbuf", [128, 4096], "bfloat16"),
    "G": ("sbuf", [128, 4096], "float16"), "X": ("sbuf", [128, 4096], "bfloat16"), "MX": ("sbuf", [128, 4096], "bfloat16"),
    "WO": ("sbuf", [128, 256 * NV], "uint16"), "WF": ("sbuf", [128, 256 * NV], "float16"), "SF": ("sbuf", [128, 256 * NV], "float16"),
    "YW": ("sbuf", [128, 256], "float32"), "F0": ("sbuf", [128, FO + 2064], "int32"),
    "EO": ("sbuf", [128, 256], "uint16"), "VT": ("sbuf", [128, 256], "float16"), "NG": ("sbuf", [128, 256], "bfloat16"),
    "MB": ("sbuf", [128, 256], "bfloat16"), "KS": ("sbuf", [128, 1024], "int32"), "KP": ("sbuf", [128, 256], "float32"),
    "PL": ("sbuf", [128, 96], "int32"), "U2": ("sbuf", [128, 16], "float32"),
    "QW": ("sbuf", [128, 128], "float16"), "QT": ("sbuf", [128, 256], "float16"),
    "DM": ("sbuf", [128, 256], "float16"), "EV": ("sbuf", [128, 256], "bfloat16"), "SS": ("sbuf", [128, 256], "bfloat16"),
    "PR": ("sbuf", [128, 256], "float16"), "EQ": ("sbuf", [128, 512], "bfloat16"),
    "TT": ("sbuf", [128, 512], "float16"), "BS": ("sbuf", [128, 512], "float32"), "SM": ("sbuf", [128, 64], "float32"),
    "LO": ("sbuf", [128, 16], "uint16"), "LG": ("sbuf", [128, 16], "uint16"),
    "OLD": ("sbuf", [128, 256], "float16"), "CL": ("sbuf", [128, 256], "float32"), "DL": ("sbuf", [128, 256], "int32"),
    "AC": ("sbuf", [128, 2], "float32"), "AR": ("sbuf", [128, 1], "float32"), "NP": ("sbuf", [128, 1], "float32"),
    "ONE": ("sbuf", [128, 128], "bfloat16"), "ODD": ("sbuf", [128, 128], "bfloat16"), "OFF": ("sbuf", [128, 128], "bfloat16"),
    "IK": ("sbuf", [128, 256], "bfloat16"), "BI": ("sbuf", [128, 16], "int32"), "BL": ("sbuf", [128, 16], "uint16"),
    "PI": ("sbuf", [128, 4], "int32"), "PF": ("sbuf", [128, 16], "float32"),
    "GM0": ("sbuf", [128, 16], "bfloat16"), "GM": ("sbuf", [128, 16], "bfloat16"), "GB": ("sbuf", [128, 8], "bfloat16"),
    "ROW": ("sbuf", [128, 912], "bfloat16"), "IDS": ("sbuf", [128, 256], "bfloat16"), "NID": ("sbuf", [128, 128], "bfloat16"),
    "CF": ("sbuf", [128, 128], "float32"), "NSH": ("sbuf", [128, 128], "bfloat16"),
    "SHF": ("sbuf", [128, 128], "bfloat16"), "REV": ("sbuf", [128, 128], "bfloat16"), "KEEP": ("sbuf", [128, 128], "bfloat16"),
    "DR": ("sbuf", [128, 128], "bfloat16"), "MK": ("sbuf", [128, 128], "bfloat16"),
    "BK0": ("sbuf", [128, 256], "bfloat16"), "BLK": ("sbuf", [128, 256], "bfloat16"),
    "TR0": ("sbuf", [128, 256], "bfloat16"), "TRI": ("sbuf", [128, 256], "bfloat16"),
    "PS": ("sbuf", [128, 96], "bfloat16"), "WT": ("sbuf", [128, 8], "bfloat16"),
    "B30": ("sbuf", [128, 8], "bfloat16"), "B31": ("sbuf", [128, 8], "bfloat16"), "B32": ("sbuf", [128, 8], "bfloat16"),
    "RST": ("sbuf", [128, 256], "bfloat16"), "CT": ("sbuf", [128, 192], "bfloat16"), "CQ": ("sbuf", [128, 512], "bfloat16"),
    "RL": ("sbuf", [128, 512], "float16"),
}
for _b in "KPMQ":
    for _c in "01":
        SCRATCH["b" + _b + _c] = ("psum", [128, 512], "float32")
SEMAPHORES = (["cV", "cA", "cP", "cG", "sent"] + ["arr%d%d" % (t, c) for t in range(1, NV) for c in range(2)]
              + ["dma%d" % i for i in range(15)])

CFG = {
    "FG": {1: "AAAA VVVV", 0: "AAAA VVVV"}, "XG": {1: "AA AA VV VV", 0: "AA AA AA VV"}, "MN": {1: "VVVV", 0: "AAAA"},
    "VS": {1: 1, 0: 1}, "HS": {1: 1, 0: 1}, "RD": 1, "NB": 3, "F0": 1, "KI": 384, "EQ": "VV", "DL": "VV",
    "WO": "VV", "VT": "AA", "EO": "VV", "QW": "VV", "QT": "AA", "LO": "AA", "OLD": "AA", "SF": "AA", "TT": "AA", "BS": "AA",
    "gam": 1.56, "sig": 3.8, "pe": 0.42, "wake": 70.0, "far": 2600.0, "far0": 2000.0, "least": 8, "visit": "", "first": "",
}


CFG.update({'FG': {1: 'VV AAAA V V', 0: 'AAAAA V V V'}, 'XG': {1: 'VV AA A VVV', 0: 'V V V A A A V A'}, 'MN': {1: 'VVVV', 0: 'AAAA'}, 'VS': {1: 1, 0: 1}, 'HS': {1: 1, 0: 1}, 'RD': 1, 'NB': 3, 'F0': 1, 'KI': 128, 'EQ': 'AV', 'DL': 'AV', 'WO': 'AV', 'VT': 'VA', 'EO': 'VA', 'QW': 'VA', 'QT': 'AA', 'LO': 'VV', 'OLD': 'VA', 'SF': 'AA', 'TT': 'AA', 'BS': 'AA'})
CFG["visit"] = 'AG1.2 VG1.0 VG1.6 keep mprev0 VWO0 mkw0 VG1.7 mkey1 AG0.0 VG0.7 mpick1 VG0.5 VVT1 VG0.6 mturn1 mtd0 mn1921 VEO1 mkw1 VNG1 AX1.2 VX1.0 mtt1 mpick0 VX1.5 ATT1 msum1.0 AVT0 AX1.4 mturn0 mke1 AEO0 VAR+ VNG0 msum1.1 AX0.7 VX0.0 VX0.1 AX0.3 mkx1.3 mtt0 VX0.2 mkx1.0 AMB1.0 mkx1.2 AX0.4 mkx1.1 VX0.6 mwide1.0 AX0.5 msum0.0 VMX1.0.0 ATT0 msum0.1 VMX1.2.0 mx0.1.0 VNP+ VMX1.3.0 AMB0.0 mu1 mkm1.0 mx0.0.0 AU21 VMX1.1.0 AKZ1 mkm1.2 msub0.0.0 mkm1.3 mkm1.1 AMX0.0.0 msub0.1.0 VKS1 mx0.2.0 VKP1 AMX0.1.0 msub0.2.0 VPL1 VPK1 VT11 VEV1 mx0.3.0 AQS1 VPC1 AMX0.2.0 msub0.3.0 VDM1 VSS1 mkm0.1 VPV1 mlo1 VGO1 AMX0.3.0 VQW1 mkm0.2 VTD1 mq1 VPR1 mke0 mkm0.0 AQT1 VLO1 VCW1 mkm0.3 VOLD1 ABW1 mwin1 mnew1 VKS0 mu0 mtri1 mover1 ASF1 VKP0 AU20 VPL0 VPK0 mblk1 send1 VT10 VDM0 AKZ0 ARL1 VPV0 VPC0 mlo0 VEV0 AQS0 mlist0 AAC1 mmend1 AQW0 VEQ1 mlist1 mq0 VSS0 ADL1 VLO0 mvoid1 VTD0 mtri0 AQT0 VGO0 mblk0 VLG1 AOLD0 VPR0 mbound0 AAC0 mwin0 Vput7 ABS0 mnew0 VCW0 VCL0 Vput6 ASF0 VEQ0 send0 Vput5 mvoid0 VDL0 mkey0- Vput4 VLG0 AWO1- mtd1- Vput3 mprev1- mback Vput2 Vput1 Vput0'
CFG["first"] = 'swi afin0 sfin1 srec srec2 gPI vONE vB300 vKC0 gGM0 vPI0 vPI1 gID vPF vNP vRST ar1 ar2 gGM vQW0 aw2 vCT aNID gODD vFe vB301 aPS1b vCF aGB vKC aCTs vC32 arow0 gSH vN192 aPS0b aCTv aCTk aPS0a aCTz gB31 aCTr aCTo gIK aNSH aCTn aWF01 vWO01 mct gKEEP vFd vRST#2 @mkey0 aFh0 vFl0 gSHF @mtd1 aFh1 vFl1 gBI gREV vTR0 aWT aCQ gOFF @AG1.2 gBK01 vDR gB32 @VG1.6 gBK00 @keep gBLK0 @mkey1 gBLK1 @mpick1 vTRI @VVT1 vBL @msum1.1 alow @mkx1.2 aPS1a @msum0.1 ahigh @mx0.0.0 vMK @mkm1.3'


def parts(text):
    out, at = [], 0
    for word in text.split():
        for i, ch in enumerate(word):
            if i and ch == word[i - 1]:
                out[-1][2] += 1
            else:
                out.append([ch, at, at + 1])
            at += 1
    return out


def build(g, T, topo, core, cfg):
    ops = []
    V, S, PE = g.vector, g.scalar, g.tensor
    gam, sig, pe = cfg["gam"], cfg["sig"], cfg["pe"]
    ndma, now = [0], [-1]

    def op(q, fn, rd, wr, cost, banks=(), lat=0.0, sem=None, cnt=0, name=None):
        ops.append({"q": q, "fn": fn, "rd": list(rd), "wr": list(wr), "cost": cost, "banks": list(banks), "lat": lat,
                    "sem": sem, "cnt": cnt, "t": now[0], "name": name})

    def call(name):
        ops[-1]["name"] = name

    def v(fn, rd, wr, n, banks=()):
        op("V", fn, rd, wr, 50 + 0.83 * max(n, cfg["least"]), banks)

    def a(fn, rd, wr, n, banks=()):
        op("A", fn, rd, wr, 65 + 0.83 * max(n, cfg["least"]), banks)

    def mm(name, lst, rd, wr, bank, least=64, group=None):
        close = [False]

        def fn():
            r = None
            for i, (o, l, rh, st, sp, n) in enumerate(lst):
                r = PE.matmul(o, l, rh, st, sp or (close[0] and i == len(lst) - 1))
            return r
        op("P", fn, rd, list(wr) + ([] if group else ["order " + bank]), sum(max(least, m[5]) * pe + 3 for m in lst), [bank], 60.0,
           name="m" + name)
        ops[-1]["group"], ops[-1]["close"] = group, close

    def dma(q, out, in_, rd, wr, lat):
        e = {"S": g.sync, "A": g.scalar}[q]
        op(q, lambda: e.dma_start(out, in_), rd, wr, 60, (), lat, "dma%d" % ndma[0], 16)
        ndma[0] += 1

    def ts(o, i, s1, s2, o0, o1=None):
        if o1 is None:
            return lambda: V.tensor_scalar(o, i, s1, None, o0)
        return lambda: V.tensor_scalar(o, i, s1, s2, o0, o1)

    def tt(o, i0, i1, o0):
        return lambda: V.tensor_tensor(o, i0, i1, o0)

    def cp(o, i):
        return lambda: V.tensor_copy(o, i)

    def ms(o, c):
        return lambda: V.memset(o, c)

    def act(o, i, f, **kw):
        return lambda: S.activation(o, i, f, **kw)

    def scan(o, d0, d1, o0, o1):
        return lambda: V.tensor_tensor_scan(o, d0, d1, 0.0, o0, o1)

    def iota(o, key, pat, cm, n, flag=True):
        if flag:
            op("G", lambda: g.iota(o, pat, 0, cm, allow_small_or_imprecise_dtypes=True), [], [key], 130 + 1.66 * n)
        else:
            op("G", lambda: g.iota(o, pat, 0, cm), [], [key], 130 + 1.66 * n)

    def sel(o, key, i, rd, pat, cmp, base, cm, n=128, fill=0.0):
        op("G", lambda: g.affine_select(o, i, pat, cmp, fill, base, cm), rd, [key], 170 + 1.66 * n)

    def plus(who, out, in_, add, rd, wr, n, banks=(), half=False):
        if who == "A":
            a(act(out, in_, AF.Identity, bias=add) if add else act(out, in_, AF.Copy), rd, wr, n, banks)
        else:
            v(ts(out, in_, add, None, A.add) if add else cp(out, in_), rd, wr, n / 2 if half else n, banks)

    def gather(who, out, win, rd, wr, n):
        if who == "V":
            v(cp(out, win), rd, wr, gam * n)
        else:
            a(act(out, win, AF.Copy), rd, wr, gam * n)

    dma("S", T.wi[:], T.wnd[:], [], ["wi"], 2200)
    dma("A", T.fin[:, 0:512], T.fld[:, 0:512], [], ["fin0"], 2700)
    dma("S", T.fin[:, 512:1024], T.fld[:, 512:1024], [], ["fin1"], 3200)
    dma("S", T.R[:, 0:2048], T.rec[:], [], ["rec"], 4400)
    if cfg["RD"]:
        dma("S", T.R[:, 2048:4096], T.rec[:], [], ["rec2"], 5600)
    ID, SH, ONE = T.IDS[:, 128:256], T.IDS[:, 0:128], T.ONE[0:1, :]
    N192, KC, C32 = T.ROW[0:1, 0:512], T.ROW[0:1, 512:896], T.ROW[0:1, 896:904]
    v(ms(T.ONE[:], 1.0), [], ["ONE"], 64)
    for key, lo, hi, val in (("N192", 0, 512, -192.0), ("KC0", 512, 768, 0.0), ("KC", 768, 896, -65536.0), ("C32", 896, 912, FO + 0.0)):
        v(ms(T.ROW[0:32, lo:hi], val), [], [key], (hi - lo) / 2)
    v(ms(T.F[:, 0:FO], 0), [], ["Fd"], 32)
    v(ms(T.F[:, FO + 2048:FO + 2064], 0), [], ["Fe"], 16)
    v(ms(T.NP[:], 0.0), [], ["NP"], 8)
    v(ms(T.CF[:], 1.0), [], ["CF"], 128)
    v(ms(T.CT[:], 0.0), [], ["CT"], 96)
    v(ms(T.RST[:], 2048.0), [], ["RST"], 128)
    v(ms(T.RST[:, 0:256:16], -2.0 ** 26), [], ["RST"], 16)
    v(ms(T.QW[:], 1.0), [], ["QW0", "QW1", "QS0", "QS1"], 64)
    for h in range(2):
        v(ms(T.B30[:, 4 * h:4 * h + 4], 8192.0 * h - 4096.0), [], ["B30%d" % h], 8)
    iota(T.PI[:, 0:1], "PI", [[0, 1]], 1, 1, False)
    sel(ID, "ID", T.ONE[:], ["ONE"], [[-1, 128]], A.is_equal, 0, 1)
    iota(T.ODD[:], "ODD", [[0, 64], [1, 2]], 0, 128)
    sel(SH, "SH", T.ODD[:], ["ODD"], [[-1, 128]], A.is_equal, 1, 1)
    sel(T.GM0[:], "GM0", T.ONE[:, 0:16], ["ONE"], [[0, 2], [-16, 8]], A.is_ge, 0, 1, 16)
    sel(T.GM[:], "GM", T.GM0[:], ["GM0"], [[0, 2], [16, 8]], A.is_ge, 15, -1, 16)
    iota(T.IK[:], "IK", [[16, 2], [0, 8], [1, 16]], 0, 256)
    iota(T.BI[:], "BI", [[0, 2], [1, 8]], 0, 16, False)
    sel(T.KEEP[:], "KEEP", T.ONE[:], ["ONE"], [[0, 8], [1, 16]], A.is_gt, 0, 0)
    sel(T.SHF[:], "SHF", T.KEEP[:], ["KEEP"], [[-1, 128]], A.is_equal, 1, 1)
    sel(T.REV[:], "REV", T.KEEP[:], ["KEEP"], [[-16, 8], [1, 16]], A.is_equal, -15, 1)
    sel(T.OFF[:], "OFF", T.ONE[:], ["ONE"], [[-1, 128]], A.not_equal, 0, 1)
    for h in range(2):
        s = slice(128 * h, 128 * h + 128)
        sel(T.BK0[:, s], "BK0%d" % h, T.OFF[:], ["OFF"], [[-32, 4], [0, 32]], A.is_ge, -16 * h, 1)
        sel(T.BLK[:, s], "BLK%d" % h, T.BK0[:, s], ["BK0%d" % h], [[32, 4], [0, 32]], A.is_ge, 16 * h + 15, -1)
    sel(T.B31[:], "B31", T.B30[:], ["B300", "B301"], [[0, 2], [-32, 4]], A.is_ge, 0, 1, 8)
    sel(T.B32[:], "B32", T.B31[:], ["B31"], [[0, 2], [32, 4]], A.is_ge, 31, -1, 8)
    for i, m in enumerate((15, 31)):
        v(ts(T.PI[:, i + 1:i + 2], T.PI[:, 0:1], m, None, A.bitwise_and), ["PI"], ["PI%d" % i], 8)
    v(cp(T.PF[:, 0:2], T.PI[:, 1:3]), ["PI0", "PI1"], ["PF"], 8)
    lo_, p31 = T.PF[:, 0:1], T.PF[:, 1:2]
    col = {}

    def times(out, key, src, skey, scale, bias=0.0, n=8, f=AF.Identity):
        a(act(out, src, f, scale=col.get(scale, scale), bias=bias), [skey] + [scale] * (scale in col), [key], n)

    def number(name, scale, bias, f=AF.Identity):
        col[name] = T.PF[:, 2 + len(col):3 + len(col)]
        times(col[name], name, lo_, "PF", scale, bias, f=f)
    number("w2", 2.0, 1.0)
    number("low", -1.0, FO - 2.0)
    number("high", 1.0, FO + 2048.0)
    number("r1", 2.0, -32.0)
    number("r2", -1.0, 16.0, AF.Square)
    number("row0", -1.0, 1.0, AF.Relu)
    GM = T.GM[:, 0:8]
    v(cp(T.BL[:], T.BI[:]), ["BI"], ["BL"], 16)
    v(ts(T.MK[:], T.IK[:, 0:128], lo_, None, A.is_equal), ["IK", "PF"], ["MK"], 64)
    v(ts(T.TR0[:], T.IK[:], p31, 8192.0, A.subtract, A.mult), ["IK", "PF"], ["TR0"], 128)
    v(ts(T.TRI[:], T.TR0[:], 1.0, None, A.min), ["TR0"], ["TRI"], 128)
    v(tt(T.DR[:], T.SHF[:], T.REV[:], A.subtract), ["SHF", "REV"], ["DR"], 256)
    times(T.NSH[:], "NSH", SH, "SH", -1.0, n=128)
    times(T.NID[:], "NID", ID, "ID", -1.0, n=128)
    times(T.WT[:], "WT", GM, "GM", "w2")
    times(T.GB[:], "GB", GM, "GM", 2048.0)
    mixed = any(len(set(m)) > 1 for m in cfg["MN"].values())
    for i, val in enumerate((1.0, -2.0, -1.0, 2.0)[:2 + 2 * mixed]):
        times(T.PS[:, 24 * i:24 * i + 16], "PS%da" % i, T.GM[:], "GM", val * 65536.0, n=16)
        times(T.PS[:, 24 * i + 16:24 * i + 24], "PS%db" % i, GM, "GM", -val * 65536.0)
    for key, m, q, src, scale in (("CTv", 0, QV, "GM", 1.0), ("CTo", 0, Q1, "GM", -1.0), ("CTs", 1, QS, "GB", 1.0), ("CTk", 1, QK, "GB", "r1"),
                                  ("CTr", 1, Q2, "GB", "r2"), ("CTz", 2, QZ, "GM", "row0")):
        times(T.CT[:, 64 * m + 8 * q:64 * m + 8 * q + 8], key, T[src][:, 0:8], src, scale)
        ops[-1]["rd"].append("CT")
    times(T.CT[:, 128 + 8 * Q1:136 + 8 * Q1], "CTn", T.CT[:, 128 + 8 * QZ:136 + 8 * QZ], "CTz", -1.0)
    c0, c1, c2 = (T.CT[:, 64 * m:64 * m + 56] for m in range(3))
    mm("ct", [(T.bM0[0:56, 0:128], c0, ID, True, False, 128), (T.bM0[0:56, 0:128], c1, T.NID[:], False, True, 128),
              (T.bM0[0:56, 128:256], c0, ID, True, False, 128), (T.bM0[0:56, 128:256], c1, ID, False, True, 128),
              (T.bM0[0:56, 256:384], c2, ID, True, True, 128),
              (T.bM0[0:56, 384:512], c0, T.NID[:], True, False, 128), (T.bM0[0:56, 384:512], c1, T.NID[:], False, True, 128)],
       ["CTv", "CTo", "CTs", "CTk", "CTr", "CTz", "CTn", "ID", "NID"], ["bM0"], "bM0")
    a(act(T.CQ[0:56, :], T.bM0[0:56, :], AF.Copy), ["bM0"], ["CQ"], 512, ["bM0"])
    CLO, CHI, CZ, CNH = (T.CQ[0:56, 128 * m:128 * m + 128] for m in range(4))
    for h in range(2):
        s = slice(512 * h, 512 * h + 512)
        a(act(T.F[:, FO + 1024 + 512 * h:FO + 1536 + 512 * h], T.fin[:, s], AF.Identity, bias=-1023.5 / 2048, scale=1.0 / 2048),
          ["fin%d" % h], ["Fh%d" % h], 512)
        v(ts(T.F[:, FO + 512 * h:FO + 512 * h + 512], T.fin[:, s], 2047, None, A.bitwise_and), ["fin%d" % h], ["Fl%d" % h], 512)
    v(cp(T.WO[:, 0:256], T.wi[:]), ["wi"], ["WO01", "WO00"], 256)
    a(act(T.WF[:, 0:256], T.wi[:], AF.Copy), ["wi"], ["WF01", "WF00"], 256)
    FK = ["Fd", "Fe", "Fh0", "Fh1", "Fl0", "Fl1"]
    rank = T.rank_of(core)
    dst = T.cores[(rank + 1) % len(T.cores)]
    rid, pid = topo.addr(dst, core)
    mask = topo.mask(core, dst)

    for t in range(NV):
        now[0] = t
        if cfg["F0"]:
            dma("S", T.F0[:], T.F[:], FK + ["rec", "rec2", "WF%d0" % t], ["F0"], 6000)
            call("keep")
        for c in (1, 0):
            C = str(c)
            w0, x0, g0, k0, p0, q0 = 256 * t + 128 * c, 128 * c, 2048 * c, 512 * c, 48 * c, 64 * c
            x = slice(x0, x0 + 128)
            c8 = slice(8 * c, 8 * c + 8)
            WFk, WOk = "WF%d%d" % (t, c), "WO%d%d" % (t, c)
            Wf = T.WF[:, w0:w0 + 128]
            BK, BP, BM, BQ = ("b" + b + C for b in "KPMQ")
            bK, bP, bM, bQ = T[BK], T[BP], T[BM], T[BQ]
            Gk = ["G%d.%d" % (c, s) for s in range(8)]
            Xk = ["X%d.%d" % (c, s) for s in range(8)]

            def who(kind, c=c):
                return cfg[kind][1 - c]
            if t:
                plus(who("WO"), T.WO[:, w0:w0 + 128], Wf, 0.0, [WFk], [WOk], 128, half=True)
                call(who("WO") + "WO" + C)
            for e, lo, hi in parts(cfg["FG"][c]):
                gather(e, T.G[:, g0 + 256 * lo:g0 + 256 * hi], T.F[:, FO:FO + 2048].indirect(T.WO[:, w0 + 16 * lo:w0 + 16 * hi]),
                       FK + [WOk], Gk[lo:hi], 256 * (hi - lo))
            mm("prev" + C, [(bP[:, 0:128], Wf, T.NSH[:], True, False, 128)], [WFk, "NSH"], [BP + "v"], BP)
            vs = cfg["VS"][c]
            for s in range(vs):
                m = 128 // vs
                mm("pick" + C, [(bP[m * s:m * s + m, k:128:16], T.G[:, g0 + 16 * m * s + k:g0 + 16 * m * (s + 1):16], ID[:, k:128:16], False,
                                 k == 15, 8) for k in range(16)], Gk[8 // vs * s:8 // vs * (s + 1)] + ["ID"], [BP + "v"], BP, min(m, 64))
            VT, NG = T.VT[:, x], T.NG[:, x]
            plus(who("VT"), VT, bP[:, 0:128], 0.0, [BP + "v"], ["VT" + C], 128, [BP])
            v(ts(NG, VT, 0.0, 2048.0, A.is_lt, A.mult), ["VT" + C], ["NG" + C], 64)
            mm("turn" + C, [(bP[:, 128:256], VT, ID, True, cfg["RD"] == 1, 128)] + [(bP[:, 128:256], NG, ID, False, True, 128)] * (1 - cfg["RD"]),
               ["VT" + C, "ID"] + ["NG" + C] * (1 - cfg["RD"]), [BP + "e"], BP)
            plus(who("EO"), T.EO[:, x], bP[:, 128:256], 2048.0 * cfg["RD"], [BP + "e"], ["EO" + C], 128, [BP])
            for e, lo, hi in parts(cfg["XG"][c]):
                gather(e, T.X[:, g0 + 256 * lo:g0 + 256 * hi], T.R[:, 0:2048 << cfg["RD"]].indirect(T.EO[:, x0 + 16 * lo:x0 + 16 * hi]),
                       ["rec", "rec2", "EO" + C], Xk[lo:hi], 256 * (hi - lo))
            TE, TD = T.TT[:, 2 * x0:2 * x0 + 128], T.TT[:, 2 * x0 + 128:2 * x0 + 256]
            BT = BQ if c else BM
            tk = [BQ + "s", BQ + "w"] if c else [BM]
            mm("td" + C, [(T[BT][:, 128:256], Wf, T.DR[:], True, True, 128)], ["DR", WFk], tk, BT)
            mm("tt" + C, [(T[BT][:, 0:128], ID, VT, True, False, 128), (T[BT][:, 0:128], ID, NG, False, True, 128)], ["VT" + C, "NG" + C, "ID"], tk, BT)
            plus(who("TT"), T.TT[:, 2 * x0:2 * x0 + 256], T[BT][:, 0:256], 0.0, tk, ["TT" + C, "TD" + C], 256, [BT])
            ki = cfg["KI"]
            mm("key" + C, [(bK[:, 384 - ki:384], ONE, KC[:, 384 - ki:384], True, False, ki)], ["ONE", "KC0", "KC"], [BK], BK)
            mm("kw" + C, [(bK[:, 0:256], Wf, T.IDS[:], False, False, 256)], [WFk, "SH", "ID", BK], [BK + "w"], BK, group=(t, c))
            mm("ke" + C, [(bK[:, 256:384], ID, TE, False, False, 128)], ["TT" + C, "ID", BK], [BK + "e"], BK, group=(t, c))
            mn, nh = cfg["MN"][c], cfg["HS"][c]
            m = 128 // nh
            QK_ = [BQ + s for s in ("s", "a", "w")]
            MB = T.MB[:, x]
            MBk = ["MB%d.%d" % (c, h) for h in range(nh)]
            if "V" in mn:
                mm("n192" + C, [(bM[:], ONE, N192, True, False, 512)], ["ONE", "N192"], [BM], BM)
            nr = 0
            for h in range(2):
                mm("sum%d.%d" % (c, h), [(bP[:, 256 + 64 * h:320 + 64 * h], ID, T.X[:, g0 + 1024 * h + k:g0 + 1024 * h + 1024:16], k == 0, k == 15, 64)
                                         for k in range(16)], Xk[4 * h:4 * h + 4] + ["ID"], [BP + "s%d" % h], BP)
                if h < 2 - nh:
                    continue
                h = h - 2 + nh
                MBh, Xh = MB[:, m * h:m * h + m], Xk[8 // nh * h:8 // nh * (h + 1)]
                a(act(MBh, bP[:, 256 + m * h:256 + m * h + m], AF.Identity, bias=192.0 - 15.0 / 32, scale=1.0 / 16),
                  [BP + "s0", BP + "s1"][h:h + 3 - nh], [MBk[h]], m, [BP])
                if "V" in mn:
                    mm("wide%d.%d" % (c, h), [(bM[:, 4 * m * h + s:4 * m * (h + 1):4], ID, MBh, False, s == 3 and h == nh - 1, m) for s in range(4)],
                       [MBk[h], "ID", BM], [BM + "h%d" % h], BM)
                for j in range(4):
                    Xj = T.X[:, g0 + 16 * m * h + j:g0 + 16 * m * (h + 1):4]
                    MXj = T.MX[:, g0 + 512 * j + 4 * m * h:g0 + 512 * j + 4 * m * (h + 1)]
                    MXk = "MX%d.%d.%d" % (c, j, h)
                    if mn[j] == "V":
                        v(tt(MXj, Xj, bM[:, 4 * m * h:4 * m * (h + 1)], A.min), Xh + [BM, BM + "h%d" % h], [MXk], 4 * m, [BM])
                    else:
                        b = [BQ, BP if h == nh - 1 else BQ][nr % 2] if "V" in mn else ([BQ, BM, BP] if h == nh - 1 else [BQ, BM, BQ])[nr % cfg["NB"]]
                        bk = QK_ if b == BQ else [BP + s for s in ("v", "e", "s0", "s1", "u", "l", "o")] if b == BP else [b]
                        nr += 1
                        mm("x%d.%d.%d" % (c, j, h), [(T[b][:, 0:4 * m], ID, Xj, True, False, 4 * m)], Xh + ["ID"], bk, b)
                        mm("sub%d.%d.%d" % (c, j, h), [(T[b][:, s:4 * m:4], T.NID[:], MBh, False, s == 3, m) for s in range(4)],
                           [MBk[h], "NID"], bk, b)
                        a(act(MXj, T[b][:, 0:4 * m], AF.Relu if "V" in mn else AF.Abs, bias=192.0), bk, [MXk], 4 * m, [b])
            mm("u" + C, [(bP[:, 392:400], MB, T.WT[:], True, True, 8)], MBk + ["WT"], [BP + "u"], BP)
            a(act(T.U2[:, c8], bP[:, 392:400], AF.Square, bias=592.0 - 192.0 * 256), [BP + "u"], ["U2" + C], 8, [BP])
            a(act(T.KS[:, k0 + 399:k0 + 512:16], T.U2[:, c8], AF.Identity, bias=-712.4375, scale=1.0 / 32), ["U2" + C], ["KZ" + C], 8)
            for j in range(4):
                i = 0 if mn[j] == "V" else 2
                if "V" in mn:
                    mm("kx%d.%d" % (c, j), [(bK[:, k:384:16], T.X[:, g0 + k:g0 + 2048:16], T.PS[:, 24 * i:24 * i + 24], False, False, 24)
                                            for k in range(j, 16, 4)], Xk + ["PS%da" % i, "PS%db" % i, BK, BK + "w"], [BK + "x%d" % j], BK,
                       group=(t, c))
                i = i + 1 if "V" in mn else 0
                mm("km%d.%d" % (c, j), [(bK[:, j + 4 * kk:384:16], T.MX[:, g0 + 512 * j + kk:g0 + 512 * j + 512:4], T.PS[:, 24 * i:24 * i + 24],
                                         False, False, 24) for kk in range(4)],
                   ["MX%d.%d.%d" % (c, j, h) for h in range(nh)] + ["PS%da" % i, "PS%db" % i, BK, BK + "w", BK + "x%d" % j], [BK + "m%d" % j], BK,
                   group=(t, c))
            KK = [BK, BK + "w", BK + "e"] + [BK + s + str(j) for s in "xm" for j in range(4)]
            v(scan(T.KS[:, k0:k0 + 256], T.RST[:], bK[:, 128:384], A.add, A.max), ["RST"] + KK, ["KS" + C], 256, [BK])
            v(scan(T.KP[:, x], T.RST[:, 0:128], bK[:, 0:128], A.add, A.max), ["RST"] + KK, ["KP" + C], 128, [BK])
            sums = T.KS[:, k0 + 271:k0 + 384:16]
            col_, n_, z_ = (T.PL[:, p0 + 8 * i:p0 + 8 * i + 8] for i in (0, 1, 3))
            v(ts(T.PL[:, p0:p0 + 16], T.KS[:, k0 + 15:k0 + 256:16], 2047, None, A.bitwise_and), ["KS" + C], ["PL" + C], 16)
            v(tt(sums, T.KP[:, x0 + 15:x0 + 128:16], T.KS[:, k0 + 143:k0 + 256:16], A.add), ["KS" + C, "KP" + C], ["T1" + C], 16)
            v(ts(T.PL[:, p0 + 32:p0 + 40], T.KS[:, k0 + 15:k0 + 128:16], 11, 15, A.arith_shift_right, A.bitwise_and), ["KS" + C], ["PK" + C], 8)
            v(ts(T.PL[:, p0 + 16:p0 + 32], T.KS[:, k0 + 271:k0 + 512:16], 2047, None, A.bitwise_and), ["T1" + C, "KZ" + C], ["PV" + C], 16)
            v(tt(T.PL[:, p0 + 40:p0 + 48], col_, sums, A.min), ["PL" + C, "T1" + C], ["PC" + C], 16)
            QW = T.QW[:, q0:q0 + 56]
            rd = ["PV" + C, "PK" + C, "PC" + C]
            if who("QW") == "V":
                v(ts(QW[:, 0:32], T.PL[:, p0 + 16:p0 + 48], 1.0, 0.0, A.add, A.max), rd, ["QW" + C], 32)
            else:
                a(act(QW[:, 0:32], T.PL[:, p0 + 16:p0 + 48], AF.Relu, bias=1.0), rd, ["QW" + C], 32)
            a(act(QW[:, 32:40], T.PL[:, p0 + 32:p0 + 40], AF.Square, bias=1.0), ["PK" + C], ["QS" + C], 8)
            mm("q" + C, [(bQ[0:56, 0:128], QW, ID, True, True, 128)], ["QW" + C, "QS" + C, "ID"], [BQ + "s"], BQ)
            QT = T.QT[0:56, x]
            plus(who("QT"), QT, bQ[0:56, 0:128], 0.0, [BQ + "s"], ["QT" + C], 128, [BQ])
            DM, SS, OLD, PR, EQ = T.DM[:, x], T.SS[:, x], T.OLD[:, x], T.PR[:, x], T.EQ[:, 2 * x0:2 * x0 + 256]
            v(tt(DM, col_.indirect(T.BL[:, 0:8]), T.MK[:], A.mult), ["PL" + C, "BL", "MK"], ["DM" + C], gam * 128)
            mm("lo" + C, [(bP[:, 400:408], DM, GM, True, True, 8)], ["DM" + C, "GM"], [BP + "o"], BP)
            plus(who("LO"), T.LO[:, c8], bP[:, 400:408], FO + 0.0, [BP + "o"], ["LO" + C], 8, [BP])
            kept = cfg["F0"] and c == 0
            gather(who("OLD"), OLD, (T.F0 if kept else T.F)[:].indirect(T.LO[:, c8]), (["F0"] if kept else FK) + ["LO" + C], ["OLD" + C], 128)
            out, okey = (T.SF[:, w0:w0 + 128], "SF%d%d" % (t, c)) if t < NV - 1 else (T.YW[:, x], "YW" + C)
            go, cw = T.SM[:, 32 * c:32 * c + 8], T.SM[:, 32 * c + 8:32 * c + 16]
            BS = T.BS[:, 2 * x0:2 * x0 + 256]
            v(tt(T.EV[:, x], n_.indirect(T.BL[:, 0:8]), TE, A.is_equal), ["PL" + C, "BL", "TT" + C], ["EV" + C], gam * 128)
            v(scan(SS, T.KEEP[:], T.EV[:, x], A.mult, A.add), ["KEEP", "EV" + C], ["SS" + C], 64)
            v(ts(go, SS[:, 15:128:16], T.NP[:], 6.0, A.add, A.is_ge), ["SS" + C, "NP"], ["GO" + C], 8)
            v(tt(cw, QW[:, 8 * QC:8 * QC + 8], go, A.mult), ["QW" + C, "GO" + C], ["CW" + C], 16)
            v(tt(TD[:, 0:128:16], n_, z_, A.subtract), ["PL" + C, "PV" + C], ["TD" + C], 16)
            if t < NV - 1:
                a(act(T.SM[:, 32 * c + 16:32 * c + 24], go, AF.Copy, accum_out=T.AC[:, c:c + 1]), ["GO" + C], ["AC" + C], 32)
            if who("DL") == "V":
                mm("bound" + C, [(bM[:, 256:384], CLO, QT, True, True, 128), (bM[:, 384:512], CHI, QT, True, True, 128)], ["QT" + C, "CQ"],
                   [BM, BM + "h0", BM + "h1"], BM)
            v(tt(PR, go.indirect(T.BL[:, 0:8]), TD, A.mult), ["GO" + C, "BL", "TD" + C], ["PR" + C], gam * 128)
            mm("win" + C, [(bQ[:, 128:256], T.REV[:], Wf, True, False, 128), (bQ[:, 128:256], CZ, QT, False, False, 128)],
               ["REV", WFk, "QT" + C, "CQ"], [BQ + "w"], BQ)
            mm("new" + C, [(bQ[:, 128:256], PR, ID, False, True, 128)], ["PR" + C, "ID"], [BQ + "w"], BQ)
            plus(who("SF"), out, bQ[:, 128:256], 0.0, [BQ + "w"], [okey], 128, [BQ])
            call(who("SF") + "SF" + C)
            if t < NV - 1:
                arr = "arr%d%d" % (t + 1, c)
                op("G", lambda w0=w0, arr=arr: g.remote_dma(T.WF[:, w0 + 256:w0 + 384], T.SF[:, w0:w0 + 128], T.sem[arr], T.sem.sent,
                                                            pid, rid, mask),
                   [okey], ["WF%d%d" % (t + 1, c)], 300, (), cfg["far"] + cfg["far0"] * (t == 0 and c == 1), arr, -1)
            else:
                dma("S", T.yw[:, x], out, [okey], ["yw" + C], 2000)
            call("send" + C)
            mm("tri" + C, [(bK[:, 0:256], ID, T.TRI[:], True, False, 256)], ["ID", "TRI"], KK, BK)
            mm("blk" + C, [(bK[:, 128 * h:128 * h + 128], T.BLK[:, 128 * h:128 * h + 128], DM, False, h == 1, 128) for h in range(2)],
               ["DM" + C, "BLK0", "BLK1"], [BK], BK)
            if who("EQ") == "V":
                plus(who("BS"), BS, bK[:, 0:256], 0.0, [BK], ["BS" + C], 256, [BK])
                v(tt(EQ, cw.indirect(T.BL[:]), BS, A.is_equal), ["CW" + C, "BL", "BS" + C], ["EQ" + C], gam * 256)
            else:
                gather("A", BS, cw.indirect(T.BL[:]), ["CW" + C, "BL"], ["BW" + C], 256)
                v(tt(EQ, bK[:, 0:256], BS, A.is_equal), ["BW" + C, BK], ["EQ" + C], 256, [BK])
            if who("DL") == "V":
                v(tt(T.CL[:, x], bM[:, 256:384], OLD, A.max), [BM, "OLD" + C], ["CL" + C], 128, [BM])
                v(tt(T.DL[:, x], bM[:, 384:512], T.CL[:, x], A.min), [BM, "CL" + C], ["DL" + C], 128, [BM])
            else:
                RL = T.RL[:, 2 * x0:2 * x0 + 256]
                mm("over" + C, [(bM[:, 0:128], CLO, QT, True, False, 128), (bM[:, 0:128], T.NID[:], OLD, False, True, 128),
                                (bM[:, 128:256], CNH, QT, True, False, 128), (bM[:, 128:256], ID, OLD, False, True, 128)],
                   ["QT" + C, "CQ", "OLD" + C, "ID", "NID"], [BM, BM + "h0", BM + "h1"], BM)
                a(act(RL, bM[:, 0:256], AF.Relu), [BM], ["RL" + C], 256, [BM])
                mm("mend" + C, [(bM[:, 256:384], ID, OLD, True, False, 128), (bM[:, 256:384], ID, RL[:, 0:128], False, False, 128),
                                (bM[:, 256:384], T.NID[:], RL[:, 128:256], False, True, 128)], ["RL" + C, "OLD" + C, "ID", "NID"], [BM], BM)
                a(act(T.DL[:, x], bM[:, 256:384], AF.Copy), [BM], ["DL" + C], 128, [BM])
            mm("list" + C, [(bP[:, 384:392], ONE, C32, True, False, 8), (bP[:, 384:392], DM, GM, False, False, 8)], ["DM" + C, "GM", "ONE", "C32"],
               [BP + "l"], BP)
            mm("void" + C, [(bP[:, 384 + h:392:2], EQ[:, 128 * h:128 * h + 128], T.B32[:, 4 * h:4 * h + 4], False, h == 1, 4) for h in range(2)],
               ["EQ" + C, "B32"], [BP + "l"], BP)
            v(ts(T.LG[:, c8], bP[:, 384:392], col["low"], col["high"], A.max, A.min), [BP + "l", "low", "high"], ["LG" + C], 8, [BP])
        for j in range(7, -1, -1):
            v(cp(T.F[:].indirect(T.LG[:, 2 * j:2 * j + 2]), T.DL[:, 32 * j:32 * j + 32]), ["LG%d" % (j // 4), "DL%d" % (j // 4)], FK, sig * 32)
            call("Vput%d" % j)
        if t < NV - 1:
            back = T.bQ0[:, 400:401]
            mm("back", [(back, T.CF[:], T.AC[:, c:c + 1], c == 0, c == 1, 256) for c in range(2)], ["CF", "AC0", "AC1"], ["bQ0a"], "bQ0")
            v(ts(T.AR[:], back, -0.5, MAGIC, A.add, A.add), ["bQ0a"], ["AR"], 8, ["bQ0"])
            v(ts(T.NP[:], T.AR[:], MAGIC, back, A.subtract, A.subtract), ["bQ0a", "AR"], ["NP"], 8, ["bQ0"])
    now[0] = NV
    for h, b in enumerate(("bK1", "bM1", "bQ1", "bM0")):
        s = slice(256 * h, 256 * h + 256)
        keys = [b] + ([b + "s", b + "w"] if b == "bQ1" else [])
        a(act(T[b][:, 0:256], T.F[:, FO + 1024 + 256 * h:FO + 1280 + 256 * h], AF.Identity, scale=2048.0), FK, keys, 256, [b])
        v(tt(T.Y[:, s], T.F[:, FO + 256 * h:FO + 256 * h + 256], T[b][:, 0:256], A.add), FK + [b], ["Y%d" % h], 256, [b])
        dma("S", T.yf[:, s], T.Y[:, s], ["Y%d" % h], ["yf%d" % h], 2100)
    return ops


def depend(ops):
    lastw, readers, seen = {}, {}, {}
    for o in ops:
        k = o["name"] or (o["q"] if o["t"] >= 0 else o["q"].lower()) + o["wr"][0]
        seen[k, o["t"]] = seen.get((k, o["t"]), 0) + 1
        o["name"] = k + ("" if seen[k, o["t"]] == 1 else "#%d" % seen[k, o["t"]])
    for i, o in enumerate(ops):
        dep = set()
        for k in o["rd"]:
            if k in lastw:
                dep.add(lastw[k])
        for k in o["wr"]:
            if k in lastw:
                dep.add(lastw[k])
            dep.update(readers.get(k, ()))
        dep.discard(i)
        o["dep"] = dep
        for k in o["rd"]:
            readers.setdefault(k, set()).add(i)
        for k in o["wr"]:
            lastw[k] = i
            readers[k] = set()


def places(ops, visit, first):
    at = {w.rstrip("+-"): i + len(visit) * (w.count("+") - w.count("-")) for i, w in enumerate(visit)}
    ahead, here = {}, len(visit)
    for w in reversed(first):
        here = at[w[1:]] if w[0] == "@" else here - 0.001
        ahead[w] = here
    return [ahead[o["name"]] if o["t"] < 0 else o["t"] * len(visit) + at[o["name"]] if o["t"] < NV else (NV + 1) * len(visit) + i
            for i, o in enumerate(ops)]


def arrange(ops, visit, first):
    key = places(ops, visit, first)
    succ = [[] for _ in ops]
    for i, o in enumerate(ops):
        for d in o["dep"]:
            succ[d].append(i)
    left = [len(o["dep"]) for o in ops]
    ready = [i for i in range(len(ops)) if left[i] == 0]
    bank, order = {}, []
    while ready:
        i = min(ready, key=lambda j: (key[j], j))
        ready.remove(i)
        o = ops[i]
        for b in o["banks"]:
            o["dep"].update(d for q, d in bank.setdefault(b, {}).items() if q != o["q"])
            bank[b][o["q"]] = i
        o["wait"] = [d for d in o["dep"] if not o["q"] == ops[d]["q"] == "P"]
        order.append(i)
        for s in succ[i]:
            left[s] -= 1
            if left[s] == 0:
                ready.append(s)
    return order


def rank_program(g, core, T, topo):
    rank = T.rank_of(core)
    if rank is None:
        return
    ops = build(g, T, topo, core, CFG)
    depend(ops)
    order = arrange(ops, CFG["visit"].split(), CFG["first"].split())
    queue = {"V": g.vector, "A": g.scalar, "P": g.tensor, "G": g, "S": g.sync}
    pos = {i: p for p, i in enumerate(order)}
    known = {q: {} for q in queue}
    plan, signal = {}, set()
    for i in order:
        o = ops[i]
        kn = known[o["q"]]
        need = []
        for d in sorted(o["wait"], key=lambda d: -pos[d]):
            p = ops[d]
            key = p["sem"] or p["q"]
            if kn.get(key, -1) >= pos[d]:
                continue
            need.append(d)
            signal.add(d)
            if p["cnt"] >= 0:
                for k, val in p["known"].items():
                    kn[k] = max(kn.get(k, -1), val)
            kn[key] = pos[d]
        o["known"] = dict(kn)
        plan[i] = need
    last = {}
    for i in order:
        if ops[i].get("group"):
            last[ops[i]["group"]] = i
    for i in last.values():
        ops[i]["close"][0] = True
    count, total = {}, {}
    sent = 0
    for i in order:
        o = ops[i]
        for d in plan[i]:
            queue[o["q"]].wait_ge(T.sem[ops[d]["sem"] or "c" + ops[d]["q"]], count[d])
        r = o["fn"]()
        if o["sem"] is None:
            if i in signal:
                total["c" + o["q"]] = count[i] = total.get("c" + o["q"], 0) + 1
                r.then_inc(T.sem["c" + o["q"]], 1)
        else:
            if o["cnt"] > 0:
                total[o["sem"]] = count[i] = o["cnt"]
                r.then_inc(T.sem[o["sem"]], o["cnt"])
            else:
                total[o["sem"]] = count[i] = len(topo.engines(T.cores[rank - 1], core))
                sent += len(topo.engines(core, T.cores[(rank + 1) % len(T.cores)]))
    total["sent"] = sent
    for s, c in total.items():
        g.wait_ge(T.sem[s], c)
